import numpy as np, ml_dtypes
CORES = [9,25,41,57]
N = 4
BF = ml_dtypes.bfloat16
X, Y, n, ORD = 64, 64, 64, 3
def normal(rng, *shape):
    v = rng.standard_normal(shape, dtype=np.float32)
    return np.where(v < 0, np.float32(-1), np.float32(1)) * np.clip(np.abs(v), np.float32(2.0 ** -8), np.float32(3))
def setup_inputs(rng):
    q = normal(rng, N, 128, n) * np.exp2(rng.integers(-1, 2, (N, 128, 1))).astype(np.float32)
    refl = ((0.5 + rng.random((N, 128, n))) * 2.0 ** -4 * rng.choice(np.array([-1.0, 1.0]), (N, 128, n))).astype(np.float32)
    return {"px": rng.integers(0, X, (N, 8, n)).astype(np.int32), "py": rng.integers(0, Y, (N, 8, n)).astype(np.int32), "q": q.astype(np.float32), "refl": refl,
            "green": normal(rng, N, 128, X * Y).astype(BF)}
def setup_inputs_corners(rng):
    d = setup_inputs(rng)
    d["px"] = rng.choice(np.array([0, 1, X - 2, X - 1]), (N, 8, n)).astype(np.int32); d["py"] = rng.choice(np.array([0, 1, Y - 2, Y - 1]), (N, 8, n)).astype(np.int32)
    d["px"][:, :, 0] = 0; d["py"][:, :, 0] = 0; d["px"][:, :, n - 1] = X - 1; d["py"][:, :, n - 1] = Y - 1; return d
def setup_inputs_lines(rng):
    d = setup_inputs(rng)
    for g in range(8):
        if g % 2 == 0: d["px"][:, g] = rng.integers(0, X)
        else: d["py"][:, g] = rng.integers(0, Y)
    return d
def setup_inputs_heap(rng):
    d = setup_inputs(rng)
    for g in range(8):
        r = int(rng.integers(0, N)); t = (r + 1 + int(rng.integers(0, N - 1))) % N; u = (t + 1) % N
        if u == r: u = (u + 1) % N
        d["px"][r, g] = rng.integers(0, X); d["py"][r, g] = rng.integers(0, Y)
        d["px"][t, g] = d["px"][u, g]; d["py"][t, g] = d["py"][u, g]
    return d
def setup_inputs_lamp(rng):
    d = setup_inputs(rng); keep = np.zeros((N, 8), np.float32); keep[rng.integers(0, N, 8), np.arange(8)] = 1
    d["q"] = d["q"] * np.repeat(keep, 16, axis=1)[:, :, None]; d["refl"] = d["refl"] * (rng.random((N, 1, n)) < 0.5).astype(np.float32); return d
def setup_inputs_spread(rng):
    d = setup_inputs(rng); z = np.exp2(rng.integers(-6, 7, (N, 1, n))) * (rng.random((N, 1, n)) > 0.0625)
    d["q"] = (d["q"] * z).astype(np.float32); d["refl"] = d["refl"] * np.float32(2.0 ** -5)
    c = (np.exp2(rng.integers(-6, 7, (N, 1, X * Y))) * (rng.random((N, 1, X * Y)) > 0.0625)).astype(np.float32); s = np.exp2(rng.integers(-2, 2, (N, 128, 1))).astype(np.float32)
    d["green"] = (d["green"].astype(np.float32) * s * c).astype(BF); return d
def check_inputs(d):
    bad = []
    if not ((d["px"] >= 0) & (d["px"] < X)).all(): bad.append("px_range")
    if not ((d["py"] >= 0) & (d["py"] < Y)).all(): bad.append("py_range")
    for k in ("q", "refl", "green"):
        if not np.isfinite(d[k].astype(np.float32)).all(): bad.append(k + "_finite")
    return bad
def reference(px, py, q, refl, green):
    y = np.zeros((N, 128, n), np.float64); own = np.arange(n)
    for g in range(8):
        p = slice(16 * g, 16 * g + 16)
        cx = px[:, g].astype(np.int64).reshape(-1); cy = py[:, g].astype(np.int64).reshape(-1)
        off = np.abs(cx[:, None] - cx[None, :]) * Y + np.abs(cy[:, None] - cy[None, :])
        parts = []
        for s in range(N):
            m = green[s, p].astype(np.float64)[:, off[:, s * n:(s + 1) * n]]; m[:, s * n + own, own] = 0
            parts.append(m)
        M = np.concatenate(parts, axis=2)
        w = q[:, p].astype(np.float64).transpose(1, 0, 2).reshape(16, N * n); a = refl[:, p].astype(np.float64).transpose(1, 0, 2).reshape(16, N * n)
        total = np.zeros((16, N * n), np.float64)
        for o in range(ORD):
            fd = np.matmul(M, w[:, :, None])[:, :, 0]
            total = total + fd; w = a * fd
        y[:, p] = total.reshape(16, N, n).transpose(1, 0, 2)
    return {"y": y.astype(np.float32)}

@@ -1,0 +1,370 @@
+from concourse.bass import DstId, RemoteDMATransfer
+from concourse.mybir import AluOpType, ActivationFunctionType
+
+NR = 4
+F32, BF = "float32", "bfloat16"
+SCRATCH = {
+    "Gt": ("sbuf", [128, 4096], BF),
+    "Mg": ("sbuf", [128, 16384], BF),
+    "Tt": ("sbuf", [128, 16384], BF),
+    "OFF": ("sbuf", [128, 1024], "uint16"),
+    "DX": ("sbuf", [128, 4, 64, 4], BF), "RA": ("sbuf", [128, 4, 64, 4], BF), "RB": ("sbuf", [128, 4, 64, 4], BF),
+    "C8i": ("sbuf", [128, 128], "int32"), "C8b": ("sbuf", [128, 128], BF),
+    "SCi": ("sbuf", [128, 8], "int32"), "SCf": ("sbuf", [128, 8], F32),
+    "CLT": ("sbuf", [128, 4, 128], BF),
+    "ONB": ("sbuf", [128, 128], BF), "ONF": ("sbuf", [128, 128], F32),
+    "E8": ("sbuf", [128, 128], BF), "IB": ("sbuf", [128, 128], BF), "I64": ("sbuf", [128, 128], BF), "IN": ("sbuf", [128, 128], BF),
+    "IQ": ("sbuf", [128, 128], F32), "IP": ("sbuf", [128, 128], F32),
+    "QR": ("sbuf", [128, 2, 64], F32), "QP": ("sbuf", [128, 2, 64], F32), "QRT": ("sbuf", [128, 2, 64], F32),
+    "RW0": ("sbuf", [128, 12, 32], BF), "RW1": ("sbuf", [128, 12, 32], BF),
+    "PC0": ("sbuf", [128, 3, 32], BF), "PC1": ("sbuf", [128, 3, 32], BF),
+    "WW": ("sbuf", [128, 2, 32], F32), "R1": ("sbuf", [128, 2, 32], F32),
+    "AC": ("sbuf", [128, 8, 64], F32), "AD": ("sbuf", [128, 8, 64], F32),
+    "UU": ("sbuf", [128, 6, 2, 32], F32), "SS": ("sbuf", [128, 2, 64], F32), "YA": ("sbuf", [128, 64], F32),
+    "YT": ("sbuf", [128, 64], F32), "YB": ("sbuf", [128, 128], F32),
+}
+for _o in range(3):
+    SCRATCH["MSG%d" % _o] = ("sbuf", [128, 4, 64], F32)
+    SCRATCH["LA%d" % _o] = ("sbuf", [128, 4, 64], F32)
+    for _c in range(2):
+        SCRATCH["MS%d%d" % (_o, _c)] = ("sbuf", [128, 4, 32], F32)
+        SCRATCH["LD%d%d" % (_o, _c)] = ("sbuf", [128, 4, 32], F32)
+for _o in range(3):
+    del SCRATCH["MSG%d" % _o], SCRATCH["LA%d" % _o]
+for _b in range(8):
+    SCRATCH["P%d" % _b] = ("psum", [128, 512], F32)
+SEMAPHORES = ["qv", "qs", "qt", "qg", "dC", "dS", "dQ", "dG", "dY", "sent", "crd",
+              "a00", "a01", "a10", "a11", "a20", "a21"]
+
+
+def bits(es):
+    return sum(1 << e for e in es)
+
+
+def rank_program(g, core, T, topo):
+    rank = T.rank_of(core)
+    if rank is None:
+        return
+    A = AluOpType
+    COPY, ABS = ActivationFunctionType.Copy, ActivationFunctionType.Abs
+    qs = {"v": g.vector, "s": g.scalar, "t": g.tensor, "g": g, "y": g.sync}
+    sem = {"v": T.sem.qv, "s": T.sem.qs, "t": T.sem.qt, "g": T.sem.qg}
+    cnt = {"v": 0, "s": 0, "t": 0, "g": 0}
+    known = {q: {"v": 0, "s": 0, "t": 0, "g": 0} for q in qs}
+    sent = [0]
+
+    def need(q, *toks):
+        top = {}
+        for tk in toks:
+            if tk is not None:
+                top[tk[0]] = max(top.get(tk[0], 0), tk[1])
+        for p, n in top.items():
+            if known[q][p] < n:
+                qs[q].wait_ge(sem[p], n)
+                known[q][p] = n
+
+    def did(q, inst):
+        inst.then_inc(sem[q], 1)
+        cnt[q] += 1
+        return (q, cnt[q])
+
+    V, S = g.vector, g.scalar
+
+    def vcopy(out, in_, *toks):
+        need("v", *toks)
+        return did("v", V.tensor_copy(out, in_))
+
+    def vtt(out, a, b, op, *toks):
+        need("v", *toks)
+        return did("v", V.tensor_tensor(out, a, b, op))
+
+    def act(out, in_, *toks):
+        need("s", *toks)
+        return did("s", S.activation(out, in_, COPY))
+
+    def mm(out, lhsT, rhs, start, stop, *toks):
+        need("t", *toks)
+        return did("t", g.tensor.matmul(out, lhsT, rhs, start, stop))
+
+    P = [T["P%d" % b] for b in range(8)]
+    peer = {k: T.cores[(rank + k) % NR] for k in range(1, NR)}
+    RW, PC = [T.RW0, T.RW1], [T.PC0, T.PC1]
+    MS = [[T["MS%d%d" % (o, c)] for c in range(2)] for o in range(3)]
+    LD = [[T["LD%d%d" % (o, c)] for c in range(2)] for o in range(3)]
+    arr = [[T.sem["a%d%d" % (o, c)] for c in range(2)] for o in range(3)]
+
+    def send(parts, *toks):
+        need("g", *toks)
+        tr = []
+        for k, dst, src, rs, es in parts:
+            rid, pid, _ = topo.addr(peer[k])
+            tr.append(RemoteDMATransfer(dst_ids=[DstId(rid=rid, pnc=pid)], dma_engine_mask=bits(es), remote_sem=rs, src=src, dst=dst))
+            sent[0] += len(es)
+        g.remote_dma_fused(tr, local_sem=T.sem.sent)
+
+    g.sync.dma_start(T.C8i[0:8, 0:64], T.px[:, :]).then_inc(T.sem.dC, 16)
+    g.scalar.dma_start(T.C8i[0:8, 64:128], T.py[:, :]).then_inc(T.sem.dC, 16)
+    g.sync.dma_start(T.SCi[:, 0:4], T.px[:, :]).then_inc(T.sem.dS, 16)
+    g.scalar.dma_start(T.SCi[:, 4:8], T.py[:, :]).then_inc(T.sem.dS, 16)
+    g.sync.dma_start(T.Gt[:, :], T.green[:, :]).then_inc(T.sem.dG, 16)
+    g.scalar.dma_start(T.QR[:, 0, :], T.q[:, :]).then_inc(T.sem.dQ, 16)
+    g.scalar.dma_start(T.QR[:, 1, :], T.refl[:, :]).then_inc(T.sem.dQ, 16)
+
+    onb = did("v", V.memset(T.ONB[:, :], 1.0))
+    onf = did("v", V.memset(T.ONF[:, :], 1.0))
+    z0 = did("v", V.memset(RW[0][:, :, :], 0.0))
+    z1 = did("v", V.memset(RW[1][:, :, :], 0.0))
+    need("g", onb)
+    e8 = did("g", g.affine_select(T.E8[0:8, :], T.ONB[0:8, :], [[1, 128]], A.is_ge, 0.0, 0, -16))
+    need("g", e8)
+    e8 = did("g", g.affine_select(T.E8[0:8, :], T.E8[0:8, :], [[-1, 128]], A.is_ge, 0.0, 15, 16))
+    ib = did("g", g.affine_select(T.IB[:, :], T.ONB[:, :], [[-1, 128]], A.is_equal, 0.0, 0, 1))
+    need("g", onf)
+    for ah in range(2):
+        iq = did("g", g.affine_select(T.IQ[:, 64 * ah:64 * ah + 64], T.ONF[:, 0:64], [[-16, 2], [-32, 2], [-1, 16]], A.is_equal, 0.0, -64 * ah, 1))
+
+    V.wait_ge(T.sem.dC, 32)
+    c8 = vcopy(T.C8b[0:8, :], T.C8i[0:8, :])
+    for co in range(2):
+        for jj in range(4):
+            bc = mm(P[4][:, co * 64 + jj * 16:co * 64 + jj * 16 + 16], T.E8[0:8, :], T.C8b[0:8, co * 64 + jj:co * 64 + 64:4], True, True, e8, c8)
+    V.wait_ge(T.sem.dS, 32)
+    sc = vcopy(T.SCf[:, :], T.SCi[:, :])
+    clt = vcopy(T.CLT[:, 0, :], P[4][:, 0:128], bc)
+    parts, eng0 = [], 0
+    for k, ne in ((3, 2), (2, 2), (1, 4)):
+        es = topo.engines(core, peer[k])
+        parts.append((k, T.CLT[:, NR - k, :], T.CLT[:, 0, :], T.sem.crd, es[eng0:eng0 + ne]))
+        eng0 += ne
+    send(parts, clt)
+    ip = did("g", g.affine_select(T.IP[:, :], T.ONF[:, :], [[-64, 2], [-1, 16], [-16, 4]], A.is_equal, 0.0, 0, 1))
+
+    def offs_s(k0, k1, *toks):
+        need("s", *toks)
+        for jj in range(4):
+            if k1 - k0 == 1:
+                t = did("s", S.activation(T.DX[:, k0, :, jj], T.CLT[:, k0, 0:64], ABS, bias=T.SCf[:, jj:jj + 1], scale=-1.0))
+            else:
+                t = did("s", S.activation(T.DX[:, k0:k1, :, jj], T.CLT[:, k0:k1, 0:64], ABS, bias=T.SCf[:, jj:jj + 1], scale=-1.0))
+        return t
+
+    def offs_v(k0, k1, *toks):
+        need("v", *toks)
+        for jj in range(4):
+            if k1 - k0 == 1:
+                oa, ob, i0 = T.RA[:, k0, :, jj], T.RB[:, k0, :, jj], T.CLT[:, k0, 64:128]
+            else:
+                oa, ob, i0 = T.RA[:, k0:k1, :, jj], T.RB[:, k0:k1, :, jj], T.CLT[:, k0:k1, 64:128]
+            col = T.SCf[:, 4 + jj:5 + jj]
+            did("v", V.tensor_scalar(oa, i0, col, 0.0, A.subtract, A.max))
+            t = did("v", V.tensor_scalar(ob, i0, col, 0.0, A.subtract, A.min))
+        return t
+
+    def offs_t(k, ps, base, *toks):
+        need("t", *toks)
+        for jj in range(4):
+            out = ps[:, base + jj:base + 256:4]
+            mm(out, T.I64[:, :], T.DX[:, k, :, jj], True, False)
+            mm(out, T.IB[:, :], T.RA[:, k, :, jj], False, False)
+            t = mm(out, T.IN[:, :], T.RB[:, k, :, jj], False, True)
+        return t
+
+    ox = offs_s(0, 1, clt, sc)
+    need("v", ib)
+    did("v", V.tensor_scalar(T.I64[:, :], T.IB[:, :], 64.0, None, A.mult))
+    idn = did("v", V.tensor_scalar(T.IN[:, :], T.IB[:, :], -1.0, None, A.mult))
+    oy = offs_v(0, 1, clt, sc)
+    ot = offs_t(0, P[6], 0, ox, oy, idn)
+    V.wait_ge(T.sem.dQ, 32)
+    for jj in range(4):
+        qp = vcopy(T.QP[:, :, jj * 16:jj * 16 + 16], T.QR[:, :, jj:64:4])
+    off0 = vcopy(T.OFF[:, 0:256], P[6][:, 0:256], ot)
+    for i in range(2):
+        qt = mm(P[3][0:64, i * 128:i * 128 + 128], T.QP[:, i, :], T.IQ[:, :], True, True, qp, iq)
+
+    def cols(k, u0, u1):
+        return k * 4096 + u0 * 1024, k * 4096 + u1 * 1024
+
+    def win(k, u0, u1):
+        return T.Gt[:, 0:4096].indirect(T.OFF[:, k * 256 + u0 * 64:k * 256 + u1 * 64])
+
+    def gath_s(k, u0, u1, *toks):
+        a, b = cols(k, u0, u1)
+        return act(T.Mg[:, a:b], win(k, u0, u1), *toks)
+
+    def gath_v(k, u0, u1, *toks):
+        a, b = cols(k, u0, u1)
+        return vcopy(T.Mg[:, a:b], win(k, u0, u1), *toks)
+
+    def turn(k, u0, u1, *toks):
+        a, b = cols(k, u0, u1)
+        need("v", *toks)
+        if k == 0:
+            lo = 65 * 16 * u0
+            z = did("v", V.memset(T.Mg[:, lo:min(lo + 65 * 16 * (u1 - u0), 4096):65], 0.0))
+            need("v", z)
+        return did("v", V.transpose(T.Tt[:, a:b], T.Mg[:, a:b]))
+
+    S.wait_ge(T.sem.dG, 16)
+    s0a = gath_s(0, 0, 2, off0)
+
+    def place(c, *toks):
+        last = []
+        need("v", *toks)
+        need("s", *toks)
+        for a in range(4):
+            for jh in range(2):
+                ah, a2 = divmod(a, 2)
+                src = PC[c][64 * ah + 32 * jh:64 * ah + 32 * jh + 32, :, 16 * a2:16 * a2 + 16]
+                dst = RW[c][32 * a:32 * a + 32, a:12:4, 16 * jh:16 * jh + 16]
+                if a % 2 == 0 or not use_s[0]:
+                    last.append(vcopy(dst, src))
+                else:
+                    last.append(act(dst, src))
+        return last
+
+    use_s = [False]
+
+    def pieces(c, w, hi, mk=None):
+        pc = PC[c]
+        need("v", hi)
+        did("v", V.tensor_tensor(T.R1[:, c, :], w, pc[:, 0, :], A.subtract))
+        m = did("v", V.tensor_tensor(pc[:, 1, :], w, pc[:, 0, :], A.subtract))
+        lo = vtt(pc[:, 2, :], T.R1[:, c, :], pc[:, 1, :], A.subtract, m)
+        return place(c, lo)
+
+    for i in range(2):
+        for ah in range(2):
+            qe = vcopy(T.QRT[64 * ah:64 * ah + 64, i, :], P[3][0:64, i * 128 + ah * 64:i * 128 + ah * 64 + 64], qt)
+    rw = [None, None]
+    for c in range(2):
+        w = T.QRT[:, 0, 32 * c:32 * c + 32]
+        hi = vcopy(PC[c][:, 0, :], w, qe)
+        rw[c] = pieces(c, w, hi)
+    use_s[0] = True
+
+    def field(c, t0, nt, ps, p0, *toks):
+        need("t", *toks)
+        for x in range(16):
+            for jh in range(2):
+                o = jh * 32 + 16 * c + x
+                t = mm(ps[p0:p0 + nt, x:192:16], T.Tt[:, t0 * 64 + o:(t0 + nt) * 64:64], RW[c][:, :, 16 * jh + x], jh == 0, jh == 1)
+        return t
+
+    nac = [0]
+
+    def evac(o, c, ps, np_, slots, tok):
+        i = nac[0] % 8
+        nac[0] += 1
+        a, b = T.AC[0:np_, i, :], T.AD[0:np_, i, :]
+        t = vcopy(a, ps[0:np_, 0:64], tok)
+        t = vtt(b, a, ps[0:np_, 64:128], A.add, t)
+        res = {}
+        for h, k in slots:
+            for ah in range(2):
+                dst = (LD if k == 0 else MS)[o][c][64 * ah:64 * ah + 64, k, :]
+                res[k] = vtt(dst, T.AD[64 * h:64 * h + 64, i, 32 * ah:32 * ah + 32], ps[64 * h:64 * h + 64, 128 + 32 * ah:160 + 32 * ah], A.add, t)
+        return res
+
+    def msg(o, c, k, es):
+        return (k, LD[o][c][:, k, :], MS[o][c][:, k, :], arr[o][c], es)
+
+    v03 = None
+    V.wait_ge(T.sem.dG, 16)
+    v03 = gath_v(0, 3, 4, off0)
+    turn(0, 3, 4, v03)
+    S.wait_ge(T.sem.crd, 8)
+    ox = offs_s(1, 4)
+    s0b = gath_s(0, 2, 3)
+    V.wait_ge(T.sem.crd, 8)
+    oy = offs_v(1, 4)
+    o1 = offs_t(1, P[7], 0, ox, oy)
+    o2 = offs_t(2, P[7], 256)
+    o3 = offs_t(3, P[5], 0)
+    off12 = vcopy(T.OFF[:, 256:768], P[7][:, 0:512], o2)
+    off3 = vcopy(T.OFF[:, 768:1024], P[5][:, 0:256], o3)
+    s1a = gath_s(1, 0, 2, off12)
+    s1b = gath_s(1, 2, 3)
+    s2a = gath_s(2, 0, 2)
+    s2b = gath_s(2, 2, 3)
+    s3a = gath_s(3, 0, 2, off3)
+    s3b = gath_s(3, 2, 3)
+
+    turn(0, 0, 2, s0a)
+    v1 = gath_v(1, 3, 4, off12)
+    turn(0, 2, 3, s0b)
+    turn(1, 3, 4, v1)
+    turn(1, 0, 2, s1a)
+    v2 = gath_v(2, 3, 4)
+    tA = turn(1, 2, 3, s1b)
+    fA = [field(c, 0, 128, P[c], 0, tA, *rw[c]) for c in range(2)]
+    turn(2, 3, 4, v2)
+    turn(2, 0, 2, s2a)
+    v3 = gath_v(3, 3, 4, off3)
+    tB = turn(2, 2, 3, s2b)
+    fB = [field(c, 128, 64, P[2 + c], 0, tB) for c in range(2)]
+    turn(3, 3, 4, v3)
+    full = topo.engines(core, peer[1])
+    h0, h1 = full[:len(full) // 2], full[len(full) // 2:]
+    ev = [evac(0, c, P[c], 128, [(0, 0), (1, 1)], fA[c]) for c in range(2)]
+    for c in range(2):
+        send([msg(0, c, 1, full)], ev[c][1])
+    tC = turn(3, 0, 2, s3a)
+    for c in range(2):
+        field(c, 192, 32, P[4 + c], 0, tC)
+    tD = turn(3, 2, 3, s3b)
+    fD = [field(c, 224, 32, P[4 + c], 32, tD) for c in range(2)]
+    ev = [evac(0, c, P[2 + c], 64, [(0, 2)], fB[c]) for c in range(2)]
+    for c in range(2):
+        send([msg(0, c, 2, full)], ev[c][2])
+    for c in range(2):
+        e = evac(0, c, P[4 + c], 64, [(0, 3)], fD[c])
+        send([msg(0, c, 3, full)], e[3])
+
+    def receive(o, c):
+        V.wait_ge(arr[o][c], 24 if o == 0 else 16)
+        u = T.UU[:, 2 * o + c, :, :]
+        own = ("v", cnt["v"])
+        t = vtt(u, LD[o][c][:, 0:2, :], LD[o][c][:, 2:4, :], A.add, own)
+        return T.UU[:, 2 * o + c, 0, :], T.UU[:, 2 * o + c, 1, :], t
+
+    banks = {1: [(6, 7), (0, 1)], 2: [(2, 3), (4, 5)]}
+    for o in (1, 2):
+        f = []
+        for c in range(2):
+            cc = slice(32 * c, 32 * c + 32)
+            u0, u1, t = receive(o - 1, c)
+            s = vtt(T.SS[:, o - 1, cc], u0, u1, A.add, t)
+            need("v", s)
+            did("v", V.tensor_tensor(PC[c][:, 0, :], T.SS[:, o - 1, cc], T.QRT[:, 1, cc], A.mult))
+            hi = did("v", V.tensor_tensor(T.WW[:, c, :], T.SS[:, o - 1, cc], T.QRT[:, 1, cc], A.mult))
+            r = pieces(c, T.WW[:, c, :], hi)
+            bB, bA = banks[o][c]
+            fb = field(c, 128, 128, P[bB], 0, *r)
+            fa = field(c, 0, 128, P[bA], 0)
+            f.append((fb, fa))
+        if o == 2:
+            ya = vtt(T.YA[:, :], T.SS[:, 0, :], T.SS[:, 1, :], A.add)
+        for c in range(2):
+            bB, bA = banks[o][c]
+            fb, fa = f[c]
+            e = evac(o, c, P[bB], 128, [(0, 2), (1, 3)], fb)
+            send([msg(o, c, 2, h0), msg(o, c, 3, h1)], e[2], e[3])
+            e = evac(o, c, P[bA], 128, [(1, 1), (0, 0)], fa)
+            send([msg(o, c, 1, full)], e[1])
+            if o == 2:
+                vtt(LD[o][c][:, 0, :], LD[o][c][:, 0, :], T.YA[:, 32 * c:32 * c + 32], A.add, e[0])
+
+    for c in range(2):
+        u0, u1, t = receive(2, c)
+        for a2 in range(2):
+            y = vtt(T.YT[:, 32 * a2 + 16 * c:32 * a2 + 16 * c + 16], T.UU[:, 4 + c, 0, 16 * a2:16 * a2 + 16], T.UU[:, 4 + c, 1, 16 * a2:16 * a2 + 16], A.add, t)
+    yt = mm(P[7][0:64, 0:128], T.YT[:, :], T.IP[:, :], True, True, y, ip)
+    yb = vcopy(T.YB[0:64, :], P[7][0:64, 0:128], yt)
+    need("y", yb)
+    g.sync.dma_start(T.y[0:64, :], T.YB[0:64, 0:64]).then_inc(T.sem.dY, 16)
+    need("s", yb)
+    g.scalar.dma_start(T.y[64:128, :], T.YB[0:64, 64:128]).then_inc(T.sem.dY, 16)
+    g.sync.wait_ge(T.sem.dY, 32)
+    need("g", *[(q, cnt[q]) for q in cnt])
+    g.wait_ge(T.sem.sent, sent[0])

@@ -15,26 +15,21 @@ SCRATCH = {
     "ONB": ("sbuf", [128, 128], BF), "ONF": ("sbuf", [128, 128], F32),
     "E8": ("sbuf", [128, 128], BF), "IB": ("sbuf", [128, 128], BF), "I64": ("sbuf", [128, 128], BF), "IN": ("sbuf", [128, 128], BF),
     "IQ": ("sbuf", [128, 128], F32), "IP": ("sbuf", [128, 128], F32),
-    "QR": ("sbuf", [128, 2, 64], F32), "QP": ("sbuf", [128, 2, 64], F32), "QRT": ("sbuf", [128, 2, 64], F32),
-    "RW0": ("sbuf", [128, 12, 32], BF), "RW1": ("sbuf", [128, 12, 32], BF),
-    "PC0": ("sbuf", [128, 3, 32], BF), "PC1": ("sbuf", [128, 3, 32], BF),
-    "WW": ("sbuf", [128, 2, 32], F32), "R1": ("sbuf", [128, 2, 32], F32),
-    "AC": ("sbuf", [128, 8, 64], F32), "AD": ("sbuf", [128, 8, 64], F32),
-    "UU": ("sbuf", [128, 6, 2, 32], F32), "SS": ("sbuf", [128, 2, 64], F32), "YA": ("sbuf", [128, 64], F32),
+    "QR": ("sbuf", [128, 2, 64], F32), "QP": ("sbuf", [128, 2, 64], F32), "RT": ("sbuf", [128, 64], F32),
+    "RW": ("sbuf", [128, 2, 12, 32], BF),
+    "PC": ("sbuf", [128, 2, 3, 32], BF), "WW": ("sbuf", [128, 2, 32], F32), "R1": ("sbuf", [128, 2, 32], F32),
+    "MK": ("sbuf", [128, 192], F32), "SCN": ("sbuf", [128, 14, 192], F32),
+    "EA": ("sbuf", [128, 3, 64], F32), "EB": ("sbuf", [128, 3, 64], F32),
+    "SS": ("sbuf", [128, 2, 64], F32), "YA": ("sbuf", [128, 64], F32),
     "YT": ("sbuf", [128, 64], F32), "YB": ("sbuf", [128, 128], F32),
 }
 for _o in range(3):
-    SCRATCH["MSG%d" % _o] = ("sbuf", [128, 4, 64], F32)
-    SCRATCH["LA%d" % _o] = ("sbuf", [128, 4, 64], F32)
-    for _c in range(2):
-        SCRATCH["MS%d%d" % (_o, _c)] = ("sbuf", [128, 4, 32], F32)
-        SCRATCH["LD%d%d" % (_o, _c)] = ("sbuf", [128, 4, 32], F32)
-for _o in range(3):
-    del SCRATCH["MSG%d" % _o], SCRATCH["LA%d" % _o]
+    SCRATCH["MS%d" % _o] = ("sbuf", [128, 4, 64], F32)
+    SCRATCH["LD%d" % _o] = ("sbuf", [128, 4, 64], F32)
 for _b in range(8):
     SCRATCH["P%d" % _b] = ("psum", [128, 512], F32)
 SEMAPHORES = ["qv", "qs", "qt", "qg", "dC", "dS", "dQ", "dG", "dY", "sent", "crd",
-              "a00", "a01", "a10", "a11", "a20", "a21"]
+              "a00", "a01", "a10", "a11", "a20", "a21", "e0", "e10", "e11", "e20", "e21"]
 
 
 def bits(es):
@@ -56,8 +51,7 @@ def rank_program(g, core, T, topo):
     def need(q, *toks):
         top = {}
         for tk in toks:
-            if tk is not None:
-                top[tk[0]] = max(top.get(tk[0], 0), tk[1])
+            top[tk[0]] = max(top.get(tk[0], 0), tk[1])
         for p, n in top.items():
             if known[q][p] < n:
                 qs[q].wait_ge(sem[p], n)
@@ -88,10 +82,11 @@ def rank_program(g, core, T, topo):
 
     P = [T["P%d" % b] for b in range(8)]
     peer = {k: T.cores[(rank + k) % NR] for k in range(1, NR)}
-    RW, PC = [T.RW0, T.RW1], [T.PC0, T.PC1]
-    MS = [[T["MS%d%d" % (o, c)] for c in range(2)] for o in range(3)]
-    LD = [[T["LD%d%d" % (o, c)] for c in range(2)] for o in range(3)]
-    arr = [[T.sem["a%d%d" % (o, c)] for c in range(2)] for o in range(3)]
+    MS = [T["MS%d" % o] for o in range(3)]
+    LD = [T["LD%d" % o] for o in range(3)]
+    CC = [slice(0, 32), slice(32, 64)]
+    late = [[T.sem["a%d%d" % (o, c)] for c in range(2)] for o in range(3)]
+    early = {(o, c): T.sem["e%d%d" % (o, c)] for o in (1, 2) for c in range(2)}
 
     def send(parts, *toks):
         need("g", *toks)
@@ -112,8 +107,10 @@ def rank_program(g, core, T, topo):
 
     onb = did("v", V.memset(T.ONB[:, :], 1.0))
     onf = did("v", V.memset(T.ONF[:, :], 1.0))
-    z0 = did("v", V.memset(RW[0][:, :, :], 0.0))
-    z1 = did("v", V.memset(RW[1][:, :, :], 0.0))
+    did("v", V.memset(T.RW[:, :, :, :], 0.0))
+    mk = did("v", V.memset(T.MK[:, :], 1.0))
+    need("v", mk)
+    did("v", V.memset(T.MK[:, 0:192:3], 0.0))
     need("g", onb)
     e8 = did("g", g.affine_select(T.E8[0:8, :], T.ONB[0:8, :], [[1, 128]], A.is_ge, 0.0, 0, -16))
     need("g", e8)
@@ -121,7 +118,7 @@ def rank_program(g, core, T, topo):
     ib = did("g", g.affine_select(T.IB[:, :], T.ONB[:, :], [[-1, 128]], A.is_equal, 0.0, 0, 1))
     need("g", onf)
     for ah in range(2):
-        iq = did("g", g.affine_select(T.IQ[:, 64 * ah:64 * ah + 64], T.ONF[:, 0:64], [[-16, 2], [-32, 2], [-1, 16]], A.is_equal, 0.0, -64 * ah, 1))
+        iq = did("g", g.affine_select(T.IQ[:, 64 * ah:64 * ah + 64], T.ONF[:, 0:64], [[-16, 2], [-1, 16], [-32, 2]], A.is_equal, 0.0, -64 * ah, 1))
 
     V.wait_ge(T.sem.dC, 32)
     c8 = vcopy(T.C8b[0:8, :], T.C8i[0:8, :])
@@ -139,25 +136,18 @@ def rank_program(g, core, T, topo):
     send(parts, clt)
     ip = did("g", g.affine_select(T.IP[:, :], T.ONF[:, :], [[-64, 2], [-1, 16], [-16, 4]], A.is_equal, 0.0, 0, 1))
 
-    def offs_s(k0, k1, *toks):
+    def offs_s(ks, *toks):
         need("s", *toks)
         for jj in range(4):
-            if k1 - k0 == 1:
-                t = did("s", S.activation(T.DX[:, k0, :, jj], T.CLT[:, k0, 0:64], ABS, bias=T.SCf[:, jj:jj + 1], scale=-1.0))
-            else:
-                t = did("s", S.activation(T.DX[:, k0:k1, :, jj], T.CLT[:, k0:k1, 0:64], ABS, bias=T.SCf[:, jj:jj + 1], scale=-1.0))
+            t = did("s", S.activation(T.DX[:, ks, :, jj], T.CLT[:, ks, 0:64], ABS, bias=T.SCf[:, jj:jj + 1], scale=-1.0))
         return t
 
-    def offs_v(k0, k1, *toks):
+    def offs_v(ks, *toks):
         need("v", *toks)
         for jj in range(4):
-            if k1 - k0 == 1:
-                oa, ob, i0 = T.RA[:, k0, :, jj], T.RB[:, k0, :, jj], T.CLT[:, k0, 64:128]
-            else:
-                oa, ob, i0 = T.RA[:, k0:k1, :, jj], T.RB[:, k0:k1, :, jj], T.CLT[:, k0:k1, 64:128]
             col = T.SCf[:, 4 + jj:5 + jj]
-            did("v", V.tensor_scalar(oa, i0, col, 0.0, A.subtract, A.max))
-            t = did("v", V.tensor_scalar(ob, i0, col, 0.0, A.subtract, A.min))
+            did("v", V.tensor_scalar(T.RA[:, ks, :, jj], T.CLT[:, ks, 64:128], col, 0.0, A.subtract, A.max))
+            t = did("v", V.tensor_scalar(T.RB[:, ks, :, jj], T.CLT[:, ks, 64:128], col, 0.0, A.subtract, A.min))
         return t
 
     def offs_t(k, ps, base, *toks):
@@ -169,176 +159,158 @@ def rank_program(g, core, T, topo):
             t = mm(out, T.IN[:, :], T.RB[:, k, :, jj], False, True)
         return t
 
-    ox = offs_s(0, 1, clt, sc)
+    ox = offs_s(0, clt, sc)
     need("v", ib)
     did("v", V.tensor_scalar(T.I64[:, :], T.IB[:, :], 64.0, None, A.mult))
     idn = did("v", V.tensor_scalar(T.IN[:, :], T.IB[:, :], -1.0, None, A.mult))
-    oy = offs_v(0, 1, clt, sc)
+    oy = offs_v(0, clt, sc)
     ot = offs_t(0, P[6], 0, ox, oy, idn)
-    V.wait_ge(T.sem.dQ, 32)
-    for jj in range(4):
-        qp = vcopy(T.QP[:, :, jj * 16:jj * 16 + 16], T.QR[:, :, jj:64:4])
     off0 = vcopy(T.OFF[:, 0:256], P[6][:, 0:256], ot)
-    for i in range(2):
-        qt = mm(P[3][0:64, i * 128:i * 128 + 128], T.QP[:, i, :], T.IQ[:, :], True, True, qp, iq)
 
-    def cols(k, u0, u1):
-        return k * 4096 + u0 * 1024, k * 4096 + u1 * 1024
-
-    def win(k, u0, u1):
-        return T.Gt[:, 0:4096].indirect(T.OFF[:, k * 256 + u0 * 64:k * 256 + u1 * 64])
-
-    def gath_s(k, u0, u1, *toks):
-        a, b = cols(k, u0, u1)
-        return act(T.Mg[:, a:b], win(k, u0, u1), *toks)
-
-    def gath_v(k, u0, u1, *toks):
-        a, b = cols(k, u0, u1)
-        return vcopy(T.Mg[:, a:b], win(k, u0, u1), *toks)
+    def gather(q, k, u0, u1, *toks):
+        a, b = k * 4096 + u0 * 512, k * 4096 + u1 * 512
+        return (act if q == "s" else vcopy)(T.Mg[:, a:b], T.Gt[:, 0:4096].indirect(T.OFF[:, a // 16:b // 16]), *toks)
 
     def turn(k, u0, u1, *toks):
-        a, b = cols(k, u0, u1)
+        a, b = k * 4096 + u0 * 512, k * 4096 + u1 * 512
         need("v", *toks)
         if k == 0:
-            lo = 65 * 16 * u0
-            z = did("v", V.memset(T.Mg[:, lo:min(lo + 65 * 16 * (u1 - u0), 4096):65], 0.0))
+            lo = 65 * 8 * u0
+            z = did("v", V.memset(T.Mg[:, lo:min(lo + 65 * 8 * (u1 - u0), 4096):65], 0.0))
             need("v", z)
         return did("v", V.transpose(T.Tt[:, a:b], T.Mg[:, a:b]))
 
     S.wait_ge(T.sem.dG, 16)
-    s0a = gath_s(0, 0, 2, off0)
+    s0a = gather("s", 0, 0, 4, off0)
+    s0b = gather("s", 0, 4, 6)
+    S.wait_ge(T.sem.crd, 8)
+    ox = offs_s(slice(1, 4))
+    s0c = gather("s", 0, 6, 8)
 
-    def place(c, *toks):
+    def pieces(cs, w, hi, shared):
+        r1 = T.R1[:, cs, :]
+        need("v", hi)
+        did("v", V.tensor_tensor(r1, w, T.PC[:, cs, 0, :], A.subtract))
+        m = did("v", V.tensor_tensor(T.PC[:, cs, 1, :], w, T.PC[:, cs, 0, :], A.subtract))
+        lo = vtt(T.PC[:, cs, 2, :], r1, T.PC[:, cs, 1, :], A.subtract, m)
         last = []
-        need("v", *toks)
-        need("s", *toks)
+        need("v", lo)
+        if shared:
+            need("s", lo)
         for a in range(4):
             for jh in range(2):
                 ah, a2 = divmod(a, 2)
-                src = PC[c][64 * ah + 32 * jh:64 * ah + 32 * jh + 32, :, 16 * a2:16 * a2 + 16]
-                dst = RW[c][32 * a:32 * a + 32, a:12:4, 16 * jh:16 * jh + 16]
-                if a % 2 == 0 or not use_s[0]:
-                    last.append(vcopy(dst, src))
-                else:
-                    last.append(act(dst, src))
+                n0, p0 = 6 * a2 + 3 * ah, 64 * ah + 32 * jh
+                src = T.PC[p0:p0 + 32, cs, :, a2:32:2]
+                dst = T.RW[32 * a:32 * a + 32, cs, n0:n0 + 3, 16 * jh:16 * jh + 16]
+                last.append(act(dst, src) if shared and a2 else vcopy(dst, src))
         return last
 
-    use_s = [False]
-
-    def pieces(c, w, hi, mk=None):
-        pc = PC[c]
-        need("v", hi)
-        did("v", V.tensor_tensor(T.R1[:, c, :], w, pc[:, 0, :], A.subtract))
-        m = did("v", V.tensor_tensor(pc[:, 1, :], w, pc[:, 0, :], A.subtract))
-        lo = vtt(pc[:, 2, :], T.R1[:, c, :], pc[:, 1, :], A.subtract, m)
-        return place(c, lo)
-
+    V.wait_ge(T.sem.dQ, 32)
+    for jj in range(4):
+        qp = vcopy(T.QP[:, :, jj * 16:jj * 16 + 16], T.QR[:, :, jj:64:4])
     for i in range(2):
-        for ah in range(2):
-            qe = vcopy(T.QRT[64 * ah:64 * ah + 64, i, :], P[3][0:64, i * 128 + ah * 64:i * 128 + ah * 64 + 64], qt)
-    rw = [None, None]
-    for c in range(2):
-        w = T.QRT[:, 0, 32 * c:32 * c + 32]
-        hi = vcopy(PC[c][:, 0, :], w, qe)
-        rw[c] = pieces(c, w, hi)
-    use_s[0] = True
+        qt = mm(P[3][0:64, i * 128:i * 128 + 128], T.QP[:, i, :], T.IQ[:, :], True, True, qp, iq)
+    for ah in range(2):
+        vcopy(T.RT[64 * ah:64 * ah + 64, :], P[3][0:64, 128 + ah * 64:192 + ah * 64], qt)
+        for c in range(2):
+            qe = vcopy(T.WW[64 * ah:64 * ah + 64, c, :], P[3][0:64, ah * 64 + c * 32:ah * 64 + c * 32 + 32])
+    both = slice(0, 2)
+    hi = vcopy(T.PC[:, both, 0, :], T.WW[:, both, :], qe)
+    rw = pieces(both, T.WW[:, both, :], hi, False)
 
     def field(c, t0, nt, ps, p0, *toks):
         need("t", *toks)
         for x in range(16):
             for jh in range(2):
                 o = jh * 32 + 16 * c + x
-                t = mm(ps[p0:p0 + nt, x:192:16], T.Tt[:, t0 * 64 + o:(t0 + nt) * 64:64], RW[c][:, :, 16 * jh + x], jh == 0, jh == 1)
+                t = mm(ps[p0:p0 + nt, 12 * x:12 * x + 12], T.Tt[:, t0 * 64 + o:(t0 + nt) * 64:64], T.RW[:, c, :, 16 * jh + x], jh == 0, jh == 1)
         return t
+
+    def block(k, b, tok):
+        bank, p0 = ((0, 0), (0, 64), (2, 0), (4, 0))[k]
+        return [field(c, 64 * k + 32 * b, 32, P[bank + c], p0 + 32 * b, tok, *rw) for c in range(2)]
 
     nac = [0]
 
     def evac(o, c, ps, np_, slots, tok):
-        i = nac[0] % 8
+        i = nac[0]
         nac[0] += 1
-        a, b = T.AC[0:np_, i, :], T.AD[0:np_, i, :]
-        t = vcopy(a, ps[0:np_, 0:64], tok)
-        t = vtt(b, a, ps[0:np_, 64:128], A.add, t)
+        need("v", tok)
+        t = did("v", V.tensor_tensor_scan(T.SCN[0:np_, i, :], T.MK[0:np_, :], ps[0:np_, 0:192], 0.0, A.mult, A.add))
         res = {}
-        for h, k in slots:
+        for h, k, copy in slots:
             for ah in range(2):
-                dst = (LD if k == 0 else MS)[o][c][64 * ah:64 * ah + 64, k, :]
-                res[k] = vtt(dst, T.AD[64 * h:64 * h + 64, i, 32 * ah:32 * ah + 32], ps[64 * h:64 * h + 64, 128 + 32 * ah:160 + 32 * ah], A.add, t)
+                dst = (LD if k == 0 else MS)[o][64 * ah:64 * ah + 64, k, CC[c]]
+                res[k] = copy(dst, T.SCN[64 * h:64 * h + 64, i, 3 * ah + 2:192:6], t)
         return res
 
-    def msg(o, c, k, es):
-        return (k, LD[o][c][:, k, :], MS[o][c][:, k, :], arr[o][c], es)
+    def msg(o, cs, k, rs, es):
+        return (k, LD[o][:, k, cs], MS[o][:, k, cs], rs, es)
 
-    v03 = None
-    V.wait_ge(T.sem.dG, 16)
-    v03 = gath_v(0, 3, 4, off0)
-    turn(0, 3, 4, v03)
-    S.wait_ge(T.sem.crd, 8)
-    ox = offs_s(1, 4)
-    s0b = gath_s(0, 2, 3)
+    t0 = turn(0, 0, 4, s0a)
     V.wait_ge(T.sem.crd, 8)
-    oy = offs_v(1, 4)
-    o1 = offs_t(1, P[7], 0, ox, oy)
-    o2 = offs_t(2, P[7], 256)
-    o3 = offs_t(3, P[5], 0)
-    off12 = vcopy(T.OFF[:, 256:768], P[7][:, 0:512], o2)
-    off3 = vcopy(T.OFF[:, 768:1024], P[5][:, 0:256], o3)
-    s1a = gath_s(1, 0, 2, off12)
-    s1b = gath_s(1, 2, 3)
-    s2a = gath_s(2, 0, 2)
-    s2b = gath_s(2, 2, 3)
-    s3a = gath_s(3, 0, 2, off3)
-    s3b = gath_s(3, 2, 3)
+    oy = offs_v(slice(1, 4))
+    o1 = offs_t(1, P[6], 0, ox, oy, off0)
+    offs_t(2, P[7], 0)
+    o3 = offs_t(3, P[7], 256)
+    turn(0, 4, 6, s0b)
+    off1 = vcopy(T.OFF[:, 256:512], P[6][:, 0:256], o1)
+    v1 = gather("v", 1, 6, 8, off1)
+    off23 = vcopy(T.OFF[:, 512:1024], P[7][:, 0:512], o3)
+    s1a = gather("s", 1, 0, 4, off1)
+    s1b = gather("s", 1, 4, 6)
+    s2a = gather("s", 2, 0, 4, off23)
+    s2b = gather("s", 2, 4, 6)
+    s3a = gather("s", 3, 0, 4)
+    s3b = gather("s", 3, 4, 5)
 
-    turn(0, 0, 2, s0a)
-    v1 = gath_v(1, 3, 4, off12)
-    turn(0, 2, 3, s0b)
-    turn(1, 3, 4, v1)
-    turn(1, 0, 2, s1a)
-    v2 = gath_v(2, 3, 4)
-    tA = turn(1, 2, 3, s1b)
-    fA = [field(c, 0, 128, P[c], 0, tA, *rw[c]) for c in range(2)]
-    turn(2, 3, 4, v2)
-    turn(2, 0, 2, s2a)
-    v3 = gath_v(3, 3, 4, off3)
-    tB = turn(2, 2, 3, s2b)
-    fB = [field(c, 128, 64, P[2 + c], 0, tB) for c in range(2)]
-    turn(3, 3, 4, v3)
+    block(0, 0, t0)
+    block(0, 1, turn(0, 6, 8, s0c))
+    turn(1, 6, 8, v1)
+    block(1, 0, turn(1, 0, 4, s1a))
+    v2 = gather("v", 2, 6, 8, off23)
+    fA = block(1, 1, turn(1, 4, 6, s1b))
+    turn(2, 6, 8, v2)
+    v3 = gather("v", 3, 5, 8)
+    block(2, 0, turn(2, 0, 4, s2a))
+    turn(3, 5, 8, v3)
+    fB = block(2, 1, turn(2, 4, 6, s2b))
     full = topo.engines(core, peer[1])
     h0, h1 = full[:len(full) // 2], full[len(full) // 2:]
-    ev = [evac(0, c, P[c], 128, [(0, 0), (1, 1)], fA[c]) for c in range(2)]
+    ev = [evac(0, c, P[c], 128, [(1, 1, vcopy), (0, 0, vcopy)], fA[c]) for c in range(2)]
+    own = ev[1][0]
+    send([msg(0, slice(0, 64), 1, T.sem.e0, full)], ev[1][1])
+    block(3, 0, turn(3, 0, 4, s3a))
+    fD = block(3, 1, turn(3, 4, 5, s3b))
+    ev = [evac(0, c, P[2 + c], 64, [(0, 2, vcopy)], fB[c]) for c in range(2)]
+    send([msg(0, slice(0, 64), 2, T.sem.e0, full)], ev[1][2])
     for c in range(2):
-        send([msg(0, c, 1, full)], ev[c][1])
-    tC = turn(3, 0, 2, s3a)
-    for c in range(2):
-        field(c, 192, 32, P[4 + c], 0, tC)
-    tD = turn(3, 2, 3, s3b)
-    fD = [field(c, 224, 32, P[4 + c], 32, tD) for c in range(2)]
-    ev = [evac(0, c, P[2 + c], 64, [(0, 2)], fB[c]) for c in range(2)]
-    for c in range(2):
-        send([msg(0, c, 2, full)], ev[c][2])
-    for c in range(2):
-        e = evac(0, c, P[4 + c], 64, [(0, 3)], fD[c])
-        send([msg(0, c, 3, full)], e[3])
+        e = evac(0, c, P[4 + c], 64, [(0, 3, vcopy)], fD[c])
+        send([msg(0, CC[c], 3, late[0][c], full)], e[3])
 
-    def receive(o, c):
-        V.wait_ge(arr[o][c], 24 if o == 0 else 16)
-        u = T.UU[:, 2 * o + c, :, :]
-        own = ("v", cnt["v"])
-        t = vtt(u, LD[o][c][:, 0:2, :], LD[o][c][:, 2:4, :], A.add, own)
-        return T.UU[:, 2 * o + c, 0, :], T.UU[:, 2 * o + c, 1, :], t
+    mine = {}
+
+    def early_sum(o, c):
+        V.wait_ge(early[o, c], len(full))
+        t = vtt(T.EA[:, o, CC[c]], LD[o][:, 2, CC[c]], LD[o][:, 3, CC[c]], A.add)
+        return vtt(T.EB[:, o, CC[c]], T.EA[:, o, CC[c]], LD[o][:, 0, CC[c]], A.add, t, mine[o, c])
+
+    V.wait_ge(T.sem.e0, 2 * len(full))
+    t = vtt(T.EA[:, 0, :], LD[0][:, 1, :], LD[0][:, 2, :], A.add)
+    e0 = vtt(T.EB[:, 0, :], T.EA[:, 0, :], LD[0][:, 0, :], A.add, t, own)
 
     banks = {1: [(6, 7), (0, 1)], 2: [(2, 3), (4, 5)]}
     for o in (1, 2):
         f = []
         for c in range(2):
-            cc = slice(32 * c, 32 * c + 32)
-            u0, u1, t = receive(o - 1, c)
-            s = vtt(T.SS[:, o - 1, cc], u0, u1, A.add, t)
+            e = e0 if o == 1 else early_sum(1, c)
+            V.wait_ge(late[o - 1][c], len(full))
+            s = vtt(T.SS[:, o - 1, CC[c]], T.EB[:, o - 1, CC[c]], LD[o - 1][:, 3 if o == 1 else 1, CC[c]], A.add, e)
             need("v", s)
-            did("v", V.tensor_tensor(PC[c][:, 0, :], T.SS[:, o - 1, cc], T.QRT[:, 1, cc], A.mult))
-            hi = did("v", V.tensor_tensor(T.WW[:, c, :], T.SS[:, o - 1, cc], T.QRT[:, 1, cc], A.mult))
-            r = pieces(c, T.WW[:, c, :], hi)
+            did("v", V.tensor_tensor(T.PC[:, c, 0, :], T.SS[:, o - 1, CC[c]], T.RT[:, CC[c]], A.mult))
+            hi = did("v", V.tensor_tensor(T.WW[:, c, :], T.SS[:, o - 1, CC[c]], T.RT[:, CC[c]], A.mult))
+            r = pieces(c, T.WW[:, c, :], hi, True)
             bB, bA = banks[o][c]
             fb = field(c, 128, 128, P[bB], 0, *r)
             fa = field(c, 0, 128, P[bA], 0)
@@ -348,17 +320,20 @@ def rank_program(g, core, T, topo):
         for c in range(2):
             bB, bA = banks[o][c]
             fb, fa = f[c]
-            e = evac(o, c, P[bB], 128, [(0, 2), (1, 3)], fb)
-            send([msg(o, c, 2, h0), msg(o, c, 3, h1)], e[2], e[3])
-            e = evac(o, c, P[bA], 128, [(1, 1), (0, 0)], fa)
-            send([msg(o, c, 1, full)], e[1])
+            e = evac(o, c, P[bB], 128, [(0, 2, vcopy), (1, 3, act)], fb)
+            send([msg(o, CC[c], 2, early[o, c], h0), msg(o, CC[c], 3, early[o, c], h1)], e[2], e[3])
+            e = evac(o, c, P[bA], 128, [(1, 1, vcopy), (0, 0, act)], fa)
+            send([msg(o, CC[c], 1, late[o][c], full)], e[1])
+            mine[o, c] = e[0]
             if o == 2:
-                vtt(LD[o][c][:, 0, :], LD[o][c][:, 0, :], T.YA[:, 32 * c:32 * c + 32], A.add, e[0])
+                mine[o, c] = vtt(LD[o][:, 0, CC[c]], LD[o][:, 0, CC[c]], T.YA[:, CC[c]], A.add, e[0], ya)
 
     for c in range(2):
-        u0, u1, t = receive(2, c)
+        e = early_sum(2, c)
+        V.wait_ge(late[2][c], len(full))
         for a2 in range(2):
-            y = vtt(T.YT[:, 32 * a2 + 16 * c:32 * a2 + 16 * c + 16], T.UU[:, 4 + c, 0, 16 * a2:16 * a2 + 16], T.UU[:, 4 + c, 1, 16 * a2:16 * a2 + 16], A.add, t)
+            cs = slice(32 * c + a2, 32 * c + 32, 2)
+            y = vtt(T.YT[:, 32 * a2 + 16 * c:32 * a2 + 16 * c + 16], T.EB[:, 2, cs], LD[2][:, 1, cs], A.add, e)
     yt = mm(P[7][0:64, 0:128], T.YT[:, :], T.IP[:, :], True, True, y, ip)
     yb = vcopy(T.YB[0:64, :], P[7][0:64, 0:128], yt)
     need("y", yb)

@@ -3,21 +3,29 @@ from concourse.mybir import AluOpType, ActivationFunctionType
 
 NR = 4
 F32, BF = "float32", "bfloat16"
+SPLAN = [("gather", 0, 0, 2), ("gather", 0, 2, 3), ("places", 1, 1, 2), ("places", 2, 2, 4), ("gather", 1, 2, 6), ("gather", 2, 0, 5),
+         ("gather", 3, 3, 8), ("gather", 3, 0, 3), ("gather", 0, 5, 8)]
+VPLAN = [("gather", 0, 3, 5), ("places", 1, 1, 2), ("turn", 0, 0, 3), ("offsets", 1, 1, 2), ("list", 1, 1, 2), ("places", 2, 2, 4),
+         ("offsets", 2, 2, 4), ("gather", 1, 0, 2), ("list", 2, 2, 4), ("gather", 1, 6, 8), ("turn", 0, 3, 5), ("turn", 1, 0, 8),
+         ("gather", 2, 5, 8), ("turn", 2, 0, 5), ("turn", 2, 5, 8), ("turn", 3, 4, 8), ("evac", 1, 0, 0), ("evac", 1, 1, 0),
+         ("turn", 3, 0, 4), ("evac", 3, 0, 0), ("turn", 0, 5, 8), ("evac", 3, 1, 0)]
+COPIERS = {"12": ["gv", "gv"], "3": "vv", "fb": ["vs", "vs"], "fa": ["vs", "vs"]}
 SCRATCH = {
     "Gt": ("sbuf", [128, 4096], BF),
     "Mg": ("sbuf", [128, 16384], BF),
     "Tt": ("sbuf", [128, 16384], BF),
     "OFF": ("sbuf", [128, 1024], "uint16"),
-    "DX": ("sbuf", [128, 4, 64, 4], BF), "RA": ("sbuf", [128, 4, 64, 4], BF), "RB": ("sbuf", [128, 4, 64, 4], BF),
+    "DX": ("sbuf", [128, 4, 64, 4], BF), "RA": ("sbuf", [128, 4, 64, 4], BF),
     "C8i": ("sbuf", [128, 128], "int32"), "C8b": ("sbuf", [128, 128], BF),
-    "SCi": ("sbuf", [128, 8], "int32"), "SCf": ("sbuf", [128, 8], F32),
+    "SCf": ("sbuf", [128, 12], F32),
     "CLT": ("sbuf", [128, 4, 128], BF),
-    "ONB": ("sbuf", [128, 128], BF), "ONF": ("sbuf", [128, 128], F32),
-    "E8": ("sbuf", [128, 128], BF), "IB": ("sbuf", [128, 128], BF), "I64": ("sbuf", [128, 128], BF), "IN": ("sbuf", [128, 128], BF),
+    "ONB": ("sbuf", [128, 144], BF), "ONF": ("sbuf", [128, 128], F32),
+    "E8": ("sbuf", [128, 128], BF), "Z8": ("sbuf", [128, 144], BF),
+    "IB": ("sbuf", [128, 128], BF), "I64": ("sbuf", [128, 128], BF), "I2": ("sbuf", [128, 128], BF), "IN": ("sbuf", [128, 128], BF),
     "IQ": ("sbuf", [128, 128], F32), "IP": ("sbuf", [128, 128], F32),
-    "QR": ("sbuf", [128, 2, 64], F32), "QP": ("sbuf", [128, 2, 64], F32), "RT": ("sbuf", [128, 64], F32),
-    "RW": ("sbuf", [128, 2, 12, 32], BF),
-    "PC": ("sbuf", [128, 2, 3, 32], BF), "WW": ("sbuf", [128, 2, 32], F32), "R1": ("sbuf", [128, 2, 32], F32),
+    "QR": ("sbuf", [128, 128], F32), "RT": ("sbuf", [128, 64], F32),
+    "RW": ("sbuf", [128, 12, 2, 32], BF),
+    "PC": ("sbuf", [128, 3, 64], BF), "WW": ("sbuf", [128, 64], F32), "R1": ("sbuf", [128, 64], F32),
     "MK": ("sbuf", [128, 192], F32), "SCN": ("sbuf", [128, 14, 192], F32),
     "EA": ("sbuf", [128, 3, 64], F32), "EB": ("sbuf", [128, 3, 64], F32),
     "SS": ("sbuf", [128, 2, 64], F32), "YA": ("sbuf", [128, 64], F32),
@@ -28,8 +36,8 @@ for _o in range(3):
     SCRATCH["LD%d" % _o] = ("sbuf", [128, 4, 64], F32)
 for _b in range(8):
     SCRATCH["P%d" % _b] = ("psum", [128, 512], F32)
-SEMAPHORES = ["qv", "qs", "qt", "qg", "dC", "dS", "dQ", "dG", "dY", "sent", "crd",
-              "a00", "a01", "a10", "a11", "a20", "a21", "e0", "e10", "e11", "e20", "e21"]
+SEMAPHORES = ["qv", "qs", "qt", "qg", "dC", "dQ", "dG", "dY", "sent", "crd1", "crd2",
+              "a00", "a01", "a10", "a11", "a2", "e0", "e10", "e11", "e2"]
 
 
 def bits(es):
@@ -80,13 +88,23 @@ def rank_program(g, core, T, topo):
         need("t", *toks)
         return did("t", g.tensor.matmul(out, lhsT, rhs, start, stop))
 
+    def select(out, in_, pattern, op, base, cm, *toks):
+        need("g", *toks)
+        return did("g", g.affine_select(out, in_, pattern, op, 0.0, base, cm))
+
+    def gcopy(counts):
+        return lambda out, in_, *toks: select(out, in_, [[0, n] for n in counts], A.is_ge, 0, 0, ("g", cnt["g"]), *toks)
+
     P = [T["P%d" % b] for b in range(8)]
     peer = {k: T.cores[(rank + k) % NR] for k in range(1, NR)}
     MS = [T["MS%d" % o] for o in range(3)]
     LD = [T["LD%d" % o] for o in range(3)]
     CC = [slice(0, 32), slice(32, 64)]
-    late = [[T.sem["a%d%d" % (o, c)] for c in range(2)] for o in range(3)]
-    early = {(o, c): T.sem["e%d%d" % (o, c)] for o in (1, 2) for c in range(2)}
+    ALL = slice(0, 64)
+    late = [[T.sem["a%d%d" % (o, c)] for c in range(2)] for o in range(2)]
+    early = [T.sem.e10, T.sem.e11]
+    full = topo.engines(core, peer[1])
+    h0, h1 = full[:len(full) // 2], full[len(full) // 2:]
 
     def send(parts, *toks):
         need("g", *toks)
@@ -99,42 +117,33 @@ def rank_program(g, core, T, topo):
 
     g.sync.dma_start(T.C8i[0:8, 0:64], T.px[:, :]).then_inc(T.sem.dC, 16)
     g.scalar.dma_start(T.C8i[0:8, 64:128], T.py[:, :]).then_inc(T.sem.dC, 16)
-    g.sync.dma_start(T.SCi[:, 0:4], T.px[:, :]).then_inc(T.sem.dS, 16)
-    g.scalar.dma_start(T.SCi[:, 4:8], T.py[:, :]).then_inc(T.sem.dS, 16)
     g.sync.dma_start(T.Gt[:, :], T.green[:, :]).then_inc(T.sem.dG, 16)
-    g.scalar.dma_start(T.QR[:, 0, :], T.q[:, :]).then_inc(T.sem.dQ, 16)
-    g.scalar.dma_start(T.QR[:, 1, :], T.refl[:, :]).then_inc(T.sem.dQ, 16)
+    g.scalar.dma_start(T.QR[:, 0:64], T.q[:, :]).then_inc(T.sem.dQ, 16)
+    g.scalar.dma_start(T.QR[:, 64:128], T.refl[:, :]).then_inc(T.sem.dQ, 16)
 
     onb = did("v", V.memset(T.ONB[:, :], 1.0))
     onf = did("v", V.memset(T.ONF[:, :], 1.0))
-    did("v", V.memset(T.RW[:, :, :, :], 0.0))
+    rz = did("v", V.memset(T.RW[:, :, :, :], 0.0))
     mk = did("v", V.memset(T.MK[:, :], 1.0))
     need("v", mk)
     did("v", V.memset(T.MK[:, 0:192:3], 0.0))
-    need("g", onb)
-    e8 = did("g", g.affine_select(T.E8[0:8, :], T.ONB[0:8, :], [[1, 128]], A.is_ge, 0.0, 0, -16))
-    need("g", e8)
-    e8 = did("g", g.affine_select(T.E8[0:8, :], T.E8[0:8, :], [[-1, 128]], A.is_ge, 0.0, 15, 16))
-    ib = did("g", g.affine_select(T.IB[:, :], T.ONB[:, :], [[-1, 128]], A.is_equal, 0.0, 0, 1))
-    need("g", onf)
+    e8 = select(T.E8[0:8, :], T.ONB[0:8, 0:128], [[1, 128]], A.is_ge, 0, -16, onb)
+    e8 = select(T.E8[0:8, :], T.E8[0:8, :], [[-1, 128]], A.is_ge, 15, 16, e8)
+    z8 = select(T.Z8[0:8, :], T.ONB[0:8, :], [[1, 144]], A.is_equal, -15, -16)
+    ib = select(T.IB[:, :], T.ONB[:, 0:128], [[-1, 128]], A.is_equal, 0, 1)
     for ah in range(2):
-        iq = did("g", g.affine_select(T.IQ[:, 64 * ah:64 * ah + 64], T.ONF[:, 0:64], [[-16, 2], [-1, 16], [-32, 2]], A.is_equal, 0.0, -64 * ah, 1))
+        iq = select(T.IQ[:, 64 * ah:64 * ah + 64], T.ONF[:, 0:64], [[-16, 2], [-1, 16], [-32, 2]], A.is_equal, -64 * ah, 1, onf)
 
     V.wait_ge(T.sem.dC, 32)
     c8 = vcopy(T.C8b[0:8, :], T.C8i[0:8, :])
-    for co in range(2):
-        for jj in range(4):
-            bc = mm(P[4][:, co * 64 + jj * 16:co * 64 + jj * 16 + 16], T.E8[0:8, :], T.C8b[0:8, co * 64 + jj:co * 64 + 64:4], True, True, e8, c8)
-    V.wait_ge(T.sem.dS, 32)
-    sc = vcopy(T.SCf[:, :], T.SCi[:, :])
+    bc = mm(P[4][:, 0:128], T.E8[0:8, :], T.C8b[0:8, :], True, True, e8, c8)
+    for a in range(16):
+        bs = mm(P[5][:, 0:8], T.Z8[0:8, 15 - a:143 - a], T.C8b[0:8, a:128:16], a == 0, a == 15, z8)
     clt = vcopy(T.CLT[:, 0, :], P[4][:, 0:128], bc)
-    parts, eng0 = [], 0
-    for k, ne in ((3, 2), (2, 2), (1, 4)):
-        es = topo.engines(core, peer[k])
-        parts.append((k, T.CLT[:, NR - k, :], T.CLT[:, 0, :], T.sem.crd, es[eng0:eng0 + ne]))
-        eng0 += ne
-    send(parts, clt)
-    ip = did("g", g.affine_select(T.IP[:, :], T.ONF[:, :], [[-64, 2], [-1, 16], [-16, 4]], A.is_equal, 0.0, 0, 1))
+    sc = vcopy(T.SCf[:, 0:8], P[5][:, 0:8], bs)
+    scy = did("v", V.tensor_scalar(T.SCf[:, 8:12], P[5][:, 4:8], 0.5, None, A.mult))
+    send([(3, T.CLT[:, 1, :], T.CLT[:, 0, :], T.sem.crd1, full)], clt)
+    send([(2, T.CLT[:, 2, :], T.CLT[:, 0, :], T.sem.crd2, h0), (1, T.CLT[:, 3, :], T.CLT[:, 0, :], T.sem.crd2, h1)])
 
     def offs_s(ks, *toks):
         need("s", *toks)
@@ -145,9 +154,7 @@ def rank_program(g, core, T, topo):
     def offs_v(ks, *toks):
         need("v", *toks)
         for jj in range(4):
-            col = T.SCf[:, 4 + jj:5 + jj]
-            did("v", V.tensor_scalar(T.RA[:, ks, :, jj], T.CLT[:, ks, 64:128], col, 0.0, A.subtract, A.max))
-            t = did("v", V.tensor_scalar(T.RB[:, ks, :, jj], T.CLT[:, ks, 64:128], col, 0.0, A.subtract, A.min))
+            t = did("v", V.tensor_scalar(T.RA[:, ks, :, jj], T.CLT[:, ks, 64:128], T.SCf[:, 4 + jj:5 + jj], T.SCf[:, 8 + jj:9 + jj], A.max, A.subtract))
         return t
 
     def offs_t(k, ps, base, *toks):
@@ -155,17 +162,44 @@ def rank_program(g, core, T, topo):
         for jj in range(4):
             out = ps[:, base + jj:base + 256:4]
             mm(out, T.I64[:, :], T.DX[:, k, :, jj], True, False)
-            mm(out, T.IB[:, :], T.RA[:, k, :, jj], False, False)
-            t = mm(out, T.IN[:, :], T.RB[:, k, :, jj], False, True)
+            mm(out, T.I2[:, :], T.RA[:, k, :, jj], False, False)
+            t = mm(out, T.IN[:, :], T.CLT[:, k, 64:128], False, True)
         return t
 
     ox = offs_s(0, clt, sc)
+    oy = offs_v(0, clt, sc, scy)
     need("v", ib)
     did("v", V.tensor_scalar(T.I64[:, :], T.IB[:, :], 64.0, None, A.mult))
+    did("v", V.tensor_scalar(T.I2[:, :], T.IB[:, :], 2.0, None, A.mult))
     idn = did("v", V.tensor_scalar(T.IN[:, :], T.IB[:, :], -1.0, None, A.mult))
-    oy = offs_v(0, clt, sc)
     ot = offs_t(0, P[6], 0, ox, oy, idn)
     off0 = vcopy(T.OFF[:, 0:256], P[6][:, 0:256], ot)
+
+    def pieces(cols, hi, copiers):
+        r1, w = T.R1[:, cols], T.WW[:, cols]
+        need("v", hi)
+        m = did("v", V.tensor_tensor(T.PC[:, 1, cols], w, T.PC[:, 0, cols], A.subtract))
+        r = did("v", V.tensor_tensor(r1, w, T.PC[:, 0, cols], A.subtract))
+        lo = vtt(T.PC[:, 2, cols], r1, T.PC[:, 1, cols], A.subtract, m, r)
+        last = []
+        for a in range(4):
+            for jh in range(2):
+                ah, a2 = divmod(a, 2)
+                n0, p0 = 6 * a2 + 3 * ah, 64 * ah + 32 * jh
+                src = T.PC[p0:p0 + 32, :, cols.start + a2:cols.stop:2]
+                dst = T.RW[32 * a:32 * a + 32, n0:n0 + 3, jh, cols.start // 2:cols.stop // 2]
+                last.append(copiers[a2](dst, src, lo))
+        return last
+
+    g.tensor.wait_ge(T.sem.dQ, 32)
+    qt = mm(P[3][:, 0:128], T.QR[:, :], T.IQ[:, :], True, True, iq)
+    for ah in range(2):
+        qe = vcopy(T.WW[64 * ah:64 * ah + 64, :], P[3][0:64, ah * 64:ah * 64 + 64], qt)
+    hi = vcopy(T.PC[:, 0, :], T.WW[:, :], qe)
+    rw = pieces(ALL, hi, [gcopy([3, 32])] * 2) + [rz]
+    for ah in range(2):
+        vcopy(T.RT[64 * ah:64 * ah + 64, :], P[3][64:128, ah * 64:ah * 64 + 64])
+    ip = select(T.IP[:, :], T.ONF[:, :], [[-64, 2], [-1, 64]], A.is_equal, 0, 1, *rw)
 
     def gather(q, k, u0, u1, *toks):
         a, b = k * 4096 + u0 * 512, k * 4096 + u1 * 512
@@ -180,162 +214,154 @@ def rank_program(g, core, T, topo):
             need("v", z)
         return did("v", V.transpose(T.Tt[:, a:b], T.Mg[:, a:b]))
 
-    S.wait_ge(T.sem.dG, 16)
-    s0a = gather("s", 0, 0, 4, off0)
-    s0b = gather("s", 0, 4, 6)
-    S.wait_ge(T.sem.crd, 8)
-    ox = offs_s(slice(1, 4))
-    s0c = gather("s", 0, 6, 8)
-
-    def pieces(cs, w, hi, shared):
-        r1 = T.R1[:, cs, :]
-        need("v", hi)
-        did("v", V.tensor_tensor(r1, w, T.PC[:, cs, 0, :], A.subtract))
-        m = did("v", V.tensor_tensor(T.PC[:, cs, 1, :], w, T.PC[:, cs, 0, :], A.subtract))
-        lo = vtt(T.PC[:, cs, 2, :], r1, T.PC[:, cs, 1, :], A.subtract, m)
-        last = []
-        need("v", lo)
-        if shared:
-            need("s", lo)
-        for a in range(4):
-            for jh in range(2):
-                ah, a2 = divmod(a, 2)
-                n0, p0 = 6 * a2 + 3 * ah, 64 * ah + 32 * jh
-                src = T.PC[p0:p0 + 32, cs, :, a2:32:2]
-                dst = T.RW[32 * a:32 * a + 32, cs, n0:n0 + 3, 16 * jh:16 * jh + 16]
-                last.append(act(dst, src) if shared and a2 else vcopy(dst, src))
-        return last
-
-    V.wait_ge(T.sem.dQ, 32)
-    for jj in range(4):
-        qp = vcopy(T.QP[:, :, jj * 16:jj * 16 + 16], T.QR[:, :, jj:64:4])
-    for i in range(2):
-        qt = mm(P[3][0:64, i * 128:i * 128 + 128], T.QP[:, i, :], T.IQ[:, :], True, True, qp, iq)
-    for ah in range(2):
-        vcopy(T.RT[64 * ah:64 * ah + 64, :], P[3][0:64, 128 + ah * 64:192 + ah * 64], qt)
-        for c in range(2):
-            qe = vcopy(T.WW[64 * ah:64 * ah + 64, c, :], P[3][0:64, ah * 64 + c * 32:ah * 64 + c * 32 + 32])
-    both = slice(0, 2)
-    hi = vcopy(T.PC[:, both, 0, :], T.WW[:, both, :], qe)
-    rw = pieces(both, T.WW[:, both, :], hi, False)
-
-    def field(c, t0, nt, ps, p0, *toks):
+    def field(c, t0, nt, ps, p0, *toks, xs=range(16)):
         need("t", *toks)
-        for x in range(16):
+        for x in xs:
             for jh in range(2):
                 o = jh * 32 + 16 * c + x
-                t = mm(ps[p0:p0 + nt, 12 * x:12 * x + 12], T.Tt[:, t0 * 64 + o:(t0 + nt) * 64:64], T.RW[:, c, :, 16 * jh + x], jh == 0, jh == 1)
+                t = mm(ps[p0:p0 + nt, 12 * x:12 * x + 12], T.Tt[:, t0 * 64 + o:(t0 + nt) * 64:64], T.RW[:, :, jh, 16 * c + x], jh == 0, jh == 1)
         return t
 
-    def block(k, b, tok):
-        bank, p0 = ((0, 0), (0, 64), (2, 0), (4, 0))[k]
-        return [field(c, 64 * k + 32 * b, 32, P[bank + c], p0 + 32 * b, tok, *rw) for c in range(2)]
+    def block(k, b, toks):
+        bank, p0 = ((4, 0), (0, 0), (0, 64), (2, 0))[k]
+        return [field(c, 64 * k + 32 * b, 32, P[bank + c], p0 + 32 * b, *toks, *rw) for c in range(2)]
 
     nac = [0]
 
-    def evac(o, c, ps, np_, slots, tok):
+    def scan(np_, *banks):
         i = nac[0]
         nac[0] += 1
-        need("v", tok)
-        t = did("v", V.tensor_tensor_scan(T.SCN[0:np_, i, :], T.MK[0:np_, :], ps[0:np_, 0:192], 0.0, A.mult, A.add))
+        for ps, a, b, tok in banks:
+            need("v", tok)
+            t = did("v", V.tensor_tensor_scan(T.SCN[0:np_, i, a:b], T.MK[0:np_, a:b], ps[0:np_, a:b], 0.0, A.mult, A.add))
+        return i, t
+
+    def part(i, h, ah):
+        return T.SCN[64 * h:64 * h + 64, i, 3 * ah + 2:192:6]
+
+    copier = {"v": vcopy, "s": act, "g": gcopy([32])}
+
+    def evac(o, c, banks, slots):
+        i, t = scan(64 * len(slots), *banks)
         res = {}
-        for h, k, copy in slots:
-            for ah in range(2):
-                dst = (LD if k == 0 else MS)[o][64 * ah:64 * ah + 64, k, CC[c]]
-                res[k] = copy(dst, T.SCN[64 * h:64 * h + 64, i, 3 * ah + 2:192:6], t)
+        for h, k, who in slots:
+            res[k] = [copier[who[ah]]((LD if k == 0 else MS)[o][64 * ah:64 * ah + 64, k, CC[c]], part(i, h, ah), t) for ah in range(2)]
         return res
 
     def msg(o, cs, k, rs, es):
         return (k, LD[o][:, k, cs], MS[o][:, k, cs], rs, es)
 
-    t0 = turn(0, 0, 4, s0a)
-    V.wait_ge(T.sem.crd, 8)
-    oy = offs_v(slice(1, 4))
-    o1 = offs_t(1, P[6], 0, ox, oy, off0)
-    offs_t(2, P[7], 0)
-    o3 = offs_t(3, P[7], 256)
-    turn(0, 4, 6, s0b)
-    off1 = vcopy(T.OFF[:, 256:512], P[6][:, 0:256], o1)
-    v1 = gather("v", 1, 6, 8, off1)
-    off23 = vcopy(T.OFF[:, 512:1024], P[7][:, 0:512], o3)
-    s1a = gather("s", 1, 0, 4, off1)
-    s1b = gather("s", 1, 4, 6)
-    s2a = gather("s", 2, 0, 4, off23)
-    s2b = gather("s", 2, 4, 6)
-    s3a = gather("s", 3, 0, 4)
-    s3b = gather("s", 3, 4, 5)
+    made, turned, tok, done, e12 = {}, {}, {("off", 0): off0}, {}, []
+    crd = {1: T.sem.crd1, 2: T.sem.crd2}
 
-    block(0, 0, t0)
-    block(0, 1, turn(0, 6, 8, s0c))
-    turn(1, 6, 8, v1)
-    block(1, 0, turn(1, 0, 4, s1a))
-    v2 = gather("v", 2, 6, 8, off23)
-    fA = block(1, 1, turn(1, 4, 6, s1b))
-    turn(2, 6, 8, v2)
-    v3 = gather("v", 3, 5, 8)
-    block(2, 0, turn(2, 0, 4, s2a))
-    turn(3, 5, 8, v3)
-    fB = block(2, 1, turn(2, 4, 6, s2b))
-    full = topo.engines(core, peer[1])
-    h0, h1 = full[:len(full) // 2], full[len(full) // 2:]
-    ev = [evac(0, c, P[c], 128, [(1, 1, vcopy), (0, 0, vcopy)], fA[c]) for c in range(2)]
-    own = ev[1][0]
-    send([msg(0, slice(0, 64), 1, T.sem.e0, full)], ev[1][1])
-    block(3, 0, turn(3, 0, 4, s3a))
-    fD = block(3, 1, turn(3, 4, 5, s3b))
-    ev = [evac(0, c, P[2 + c], 64, [(0, 2, vcopy)], fB[c]) for c in range(2)]
-    send([msg(0, slice(0, 64), 2, T.sem.e0, full)], ev[1][2])
-    for c in range(2):
-        e = evac(0, c, P[4 + c], 64, [(0, 3, vcopy)], fD[c])
-        send([msg(0, CC[c], 3, late[0][c], full)], e[3])
+    def share(q, plan):
+        for what, k, u0, u1 in plan:
+            if what == "gather":
+                t = gather(q, k, u0, u1, tok["off", k])
+                made.update({(k, u): t for u in range(u0, u1)})
+            elif what == "turn":
+                while any((k, u) not in made for u in range(u0, u1)):
+                    next(scalar)
+                t = turn(k, u0, u1, *[made[k, u] for u in range(u0, u1)])
+                turned.update({(k, u): t for u in range(u0, u1)})
+                for b in range(u0 // 4, (u1 + 3) // 4):
+                    toks = [turned[k, u] for u in range(4 * b, 4 * b + 4) if (k, u) in turned]
+                    if len(toks) == 4:
+                        done[k] = block(k, b, toks)
+            elif what == "places":
+                qs[q].wait_ge(crd[k], len(full))
+                tok[q, k] = (offs_s if q == "s" else offs_v)(slice(u0, u1))
+            elif what == "offsets":
+                while ("s", k) not in tok:
+                    next(scalar)
+                for i in range(u0, u1):
+                    tok["t", k] = offs_t(i, P[5 + k], 256 * (i - u0), tok["s", k], tok["v", k], off0)
+            elif what == "list":
+                t = vcopy(T.OFF[:, 256 * u0:256 * u1], P[5 + k][:, 0:256 * (u1 - u0)], tok["t", k])
+                tok.update({("off", i): t for i in range(u0, u1)})
+            elif k == 3:
+                c = u0
+                e = evac(0, c, [(P[2 + c], 0, 192, done[3][c])], [(0, 3, COPIERS["3"])])
+                send([msg(0, CC[c], 3, late[0][c], full)], *e[3])
+            else:
+                c = u0
+                e = evac(0, c, [(P[c], 0, 192, max(done[1][c], done[2][c]))], [(0, 1, COPIERS["12"][0]), (1, 2, COPIERS["12"][1])])
+                e12.extend(e[1] + e[2])
+                if len(e12) == 8:
+                    send([msg(0, ALL, 1, T.sem.e0, h0), msg(0, ALL, 2, T.sem.e0, h1)], *e12)
+            yield what
+
+    S.wait_ge(T.sem.dG, 16)
+    V.wait_ge(T.sem.dG, 16)
+    scalar = share("s", SPLAN)
+    for _ in share("v", VPLAN):
+        pass
+    for _ in scalar:
+        pass
 
     mine = {}
 
     def early_sum(o, c):
-        V.wait_ge(early[o, c], len(full))
-        t = vtt(T.EA[:, o, CC[c]], LD[o][:, 2, CC[c]], LD[o][:, 3, CC[c]], A.add)
-        return vtt(T.EB[:, o, CC[c]], T.EA[:, o, CC[c]], LD[o][:, 0, CC[c]], A.add, t, mine[o, c])
+        if o == 0:
+            i, t = scan(64, (P[4 + c], 0, 192, done[0][c]))
+            if c == 0:
+                V.wait_ge(T.sem.e0, len(full))
+                need("v", vtt(T.EA[:, 0, :], LD[0][:, 1, :], LD[0][:, 2, :], A.add))
+            need("v", t)
+            for ah in range(2):
+                r = slice(64 * ah, 64 * ah + 64)
+                e = did("v", V.tensor_tensor(T.EB[r, 0, CC[c]], T.EA[r, 0, CC[c]], part(i, 0, ah), A.add))
+            return e
+        V.wait_ge(early[c], len(full))
+        t = vtt(T.EA[:, 1, CC[c]], LD[1][:, 2, CC[c]], LD[1][:, 3, CC[c]], A.add)
+        return vtt(T.EB[:, 1, CC[c]], T.EA[:, 1, CC[c]], LD[1][:, 0, CC[c]], A.add, t, *mine[c])
 
-    V.wait_ge(T.sem.e0, 2 * len(full))
-    t = vtt(T.EA[:, 0, :], LD[0][:, 1, :], LD[0][:, 2, :], A.add)
-    e0 = vtt(T.EB[:, 0, :], T.EA[:, 0, :], LD[0][:, 0, :], A.add, t, own)
-
-    banks = {1: [(6, 7), (0, 1)], 2: [(2, 3), (4, 5)]}
+    banks = {1: [(6, 7, 0), (1, 2, 3)], 2: [(4, 5, 6), (7, 0, 1)]}
+    e0 = [early_sum(0, c) for c in range(2)]
     for o in (1, 2):
         f = []
         for c in range(2):
-            e = e0 if o == 1 else early_sum(1, c)
+            e = e0[c] if o == 1 else early_sum(1, c)
             V.wait_ge(late[o - 1][c], len(full))
             s = vtt(T.SS[:, o - 1, CC[c]], T.EB[:, o - 1, CC[c]], LD[o - 1][:, 3 if o == 1 else 1, CC[c]], A.add, e)
             need("v", s)
-            did("v", V.tensor_tensor(T.PC[:, c, 0, :], T.SS[:, o - 1, CC[c]], T.RT[:, CC[c]], A.mult))
-            hi = did("v", V.tensor_tensor(T.WW[:, c, :], T.SS[:, o - 1, CC[c]], T.RT[:, CC[c]], A.mult))
-            r = pieces(c, T.WW[:, c, :], hi, True)
-            bB, bA = banks[o][c]
-            fb = field(c, 128, 128, P[bB], 0, *r)
-            fa = field(c, 0, 128, P[bA], 0)
-            f.append((fb, fa))
-        if o == 2:
-            ya = vtt(T.YA[:, :], T.SS[:, 0, :], T.SS[:, 1, :], A.add)
-        for c in range(2):
-            bB, bA = banks[o][c]
-            fb, fa = f[c]
-            e = evac(o, c, P[bB], 128, [(0, 2, vcopy), (1, 3, act)], fb)
-            send([msg(o, CC[c], 2, early[o, c], h0), msg(o, CC[c], 3, early[o, c], h1)], e[2], e[3])
-            e = evac(o, c, P[bA], 128, [(1, 1, vcopy), (0, 0, act)], fa)
-            send([msg(o, CC[c], 1, late[o][c], full)], e[1])
-            mine[o, c] = e[0]
-            if o == 2:
-                mine[o, c] = vtt(LD[o][:, 0, CC[c]], LD[o][:, 0, CC[c]], T.YA[:, CC[c]], A.add, e[0], ya)
+            did("v", V.tensor_tensor(T.PC[:, 0, CC[c]], T.SS[:, o - 1, CC[c]], T.RT[:, CC[c]], A.mult))
+            hi = did("v", V.tensor_tensor(T.WW[:, CC[c]], T.SS[:, o - 1, CC[c]], T.RT[:, CC[c]], A.mult))
+            r = pieces(CC[c], hi, [vcopy, act])
+            bk = [P[b] for b in banks[o][c]]
+            fb = field(c, 128, 128, bk[0], 0, *r)
+            fa = [field(c, 0, 128, bk[1 + i], 0, xs=range(8 * i, 8 * i + 8)) for i in range(2)]
+            f.append(([(bk[0], 0, 192, fb)], [(bk[1 + i], 96 * i, 96 * i + 96, fa[i]) for i in range(2)]))
 
-    for c in range(2):
-        e = early_sum(2, c)
-        V.wait_ge(late[2][c], len(full))
-        for a2 in range(2):
-            cs = slice(32 * c + a2, 32 * c + 32, 2)
-            y = vtt(T.YT[:, 32 * a2 + 16 * c:32 * a2 + 16 * c + 16], T.EB[:, 2, cs], LD[2][:, 1, cs], A.add, e)
-    yt = mm(P[7][0:64, 0:128], T.YT[:, :], T.IP[:, :], True, True, y, ip)
-    yb = vcopy(T.YB[0:64, :], P[7][0:64, 0:128], yt)
+        def first(c):
+            return evac(o, c, f[c][0], [(0, 2, COPIERS["fb"][0]), (1, 3, COPIERS["fb"][1])])
+
+        def second(c):
+            return evac(o, c, f[c][1], [(1, 1, COPIERS["fa"][0]), (0, 0, COPIERS["fa"][1])])
+
+        if o == 1:
+            for c in range(2):
+                e = first(c)
+                send([msg(o, CC[c], 2, early[c], h0), msg(o, CC[c], 3, early[c], h1)], *e[2], *e[3])
+                e = second(c)
+                send([msg(o, CC[c], 1, late[o][c], full)], *e[1])
+                mine[c] = e[0]
+        else:
+            ya = vtt(T.YA[:, :], T.SS[:, 0, :], T.SS[:, 1, :], A.add)
+            e = [first(c) for c in range(2)]
+            send([msg(o, ALL, 2, T.sem.e2, h0), msg(o, ALL, 3, T.sem.e2, h1)], *e[0][2], *e[0][3], *e[1][2], *e[1][3])
+            e = [second(c) for c in range(2)]
+            send([msg(o, ALL, 1, T.sem.a2, full)], *e[0][1], *e[1][1])
+            own = vtt(LD[o][:, 0, :], LD[o][:, 0, :], T.YA[:, :], A.add, ya, *e[0][0], *e[1][0])
+
+    V.wait_ge(T.sem.e2, len(full))
+    t = vtt(T.EA[:, 2, :], LD[2][:, 2, :], LD[2][:, 3, :], A.add)
+    e = vtt(T.EB[:, 2, :], T.EA[:, 2, :], LD[2][:, 0, :], A.add, t, own)
+    V.wait_ge(T.sem.a2, len(full))
+    for a2 in range(2):
+        y = vtt(T.YT[:, 32 * a2:32 * a2 + 32], T.EB[:, 2, a2:64:2], LD[2][:, 1, a2:64:2], A.add, e)
+    yt = mm(P[7][0:64, 256:384], T.YT[:, :], T.IP[:, :], True, True, y, ip)
+    yb = vcopy(T.YB[0:64, :], P[7][0:64, 256:384], yt)
     need("y", yb)
     g.sync.dma_start(T.y[0:64, :], T.YB[0:64, 0:64]).then_inc(T.sem.dY, 16)
     need("s", yb)

from concourse.bass import DstId, RemoteDMATransfer
from concourse.mybir import AluOpType, ActivationFunctionType

NR = 4
F32, BF = "float32", "bfloat16"
SPLAN = [("gather", 0, 0, 2), ("gather", 0, 2, 3), ("places", 1, 1, 2), ("places", 2, 2, 4), ("gather", 1, 2, 6), ("gather", 2, 0, 5),
         ("gather", 3, 3, 8), ("gather", 3, 0, 3), ("gather", 0, 5, 8)]
VPLAN = [("gather", 0, 3, 5), ("places", 1, 1, 2), ("turn", 0, 0, 3), ("offsets", 1, 1, 2), ("list", 1, 1, 2), ("places", 2, 2, 4),
         ("offsets", 2, 2, 4), ("gather", 1, 0, 2), ("list", 2, 2, 4), ("gather", 1, 6, 8), ("turn", 0, 3, 5), ("turn", 1, 0, 8),
         ("gather", 2, 5, 8), ("turn", 2, 0, 5), ("turn", 2, 5, 8), ("turn", 3, 4, 8), ("evac", 1, 0, 0), ("evac", 1, 1, 0),
         ("turn", 3, 0, 4), ("evac", 3, 0, 0), ("turn", 0, 5, 8), ("evac", 3, 1, 0)]
COPIERS = {"12": ["gv", "gv"], "3": "vv", "fb": ["vs", "vs"], "fa": ["vs", "vs"]}
SCRATCH = {
    "Gt": ("sbuf", [128, 4096], BF),
    "Mg": ("sbuf", [128, 16384], BF),
    "Tt": ("sbuf", [128, 16384], BF),
    "OFF": ("sbuf", [128, 1024], "uint16"),
    "DX": ("sbuf", [128, 4, 64, 4], BF), "RA": ("sbuf", [128, 4, 64, 4], BF),
    "C8i": ("sbuf", [128, 128], "int32"), "C8b": ("sbuf", [128, 128], BF),
    "SCf": ("sbuf", [128, 12], F32),
    "CLT": ("sbuf", [128, 4, 128], BF),
    "ONB": ("sbuf", [128, 144], BF), "ONF": ("sbuf", [128, 128], F32),
    "E8": ("sbuf", [128, 128], BF), "Z8": ("sbuf", [128, 144], BF),
    "IB": ("sbuf", [128, 128], BF), "I64": ("sbuf", [128, 128], BF), "I2": ("sbuf", [128, 128], BF), "IN": ("sbuf", [128, 128], BF),
    "IQ": ("sbuf", [128, 128], F32), "IP": ("sbuf", [128, 128], F32),
    "QR": ("sbuf", [128, 128], F32), "RT": ("sbuf", [128, 64], F32),
    "RW": ("sbuf", [128, 12, 2, 32], BF),
    "PC": ("sbuf", [128, 3, 64], BF), "WW": ("sbuf", [128, 64], F32), "R1": ("sbuf", [128, 64], F32),
    "MK": ("sbuf", [128, 192], F32), "SCN": ("sbuf", [128, 14, 192], F32),
    "EA": ("sbuf", [128, 3, 64], F32), "EB": ("sbuf", [128, 3, 64], F32),
    "SS": ("sbuf", [128, 2, 64], F32), "YA": ("sbuf", [128, 64], F32),
    "YT": ("sbuf", [128, 64], F32), "YB": ("sbuf", [128, 128], F32),
}
for _o in range(3):
    SCRATCH["MS%d" % _o] = ("sbuf", [128, 4, 64], F32)
    SCRATCH["LD%d" % _o] = ("sbuf", [128, 4, 64], F32)
for _b in range(8):
    SCRATCH["P%d" % _b] = ("psum", [128, 512], F32)
SEMAPHORES = ["qv", "qs", "qt", "qg", "dC", "dQ", "dG", "dY", "sent", "crd1", "crd2",
              "a00", "a01", "a10", "a11", "a2", "e0", "e10", "e11", "e2"]


def bits(es):
    return sum(1 << e for e in es)


def rank_program(g, core, T, topo):
    rank = T.rank_of(core)
    if rank is None:
        return
    A = AluOpType
    COPY, ABS = ActivationFunctionType.Copy, ActivationFunctionType.Abs
    qs = {"v": g.vector, "s": g.scalar, "t": g.tensor, "g": g, "y": g.sync}
    sem = {"v": T.sem.qv, "s": T.sem.qs, "t": T.sem.qt, "g": T.sem.qg}
    cnt = {"v": 0, "s": 0, "t": 0, "g": 0}
    known = {q: {"v": 0, "s": 0, "t": 0, "g": 0} for q in qs}
    sent = [0]

    def need(q, *toks):
        top = {}
        for tk in toks:
            top[tk[0]] = max(top.get(tk[0], 0), tk[1])
        for p, n in top.items():
            if known[q][p] < n:
                qs[q].wait_ge(sem[p], n)
                known[q][p] = n

    def did(q, inst):
        inst.then_inc(sem[q], 1)
        cnt[q] += 1
        return (q, cnt[q])

    V, S = g.vector, g.scalar

    def vcopy(out, in_, *toks):
        need("v", *toks)
        return did("v", V.tensor_copy(out, in_))

    def vtt(out, a, b, op, *toks):
        need("v", *toks)
        return did("v", V.tensor_tensor(out, a, b, op))

    def act(out, in_, *toks):
        need("s", *toks)
        return did("s", S.activation(out, in_, COPY))

    def mm(out, lhsT, rhs, start, stop, *toks):
        need("t", *toks)
        return did("t", g.tensor.matmul(out, lhsT, rhs, start, stop))

    def select(out, in_, pattern, op, base, cm, *toks):
        need("g", *toks)
        return did("g", g.affine_select(out, in_, pattern, op, 0.0, base, cm))

    def gcopy(counts):
        return lambda out, in_, *toks: select(out, in_, [[0, n] for n in counts], A.is_ge, 0, 0, ("g", cnt["g"]), *toks)

    P = [T["P%d" % b] for b in range(8)]
    peer = {k: T.cores[(rank + k) % NR] for k in range(1, NR)}
    MS = [T["MS%d" % o] for o in range(3)]
    LD = [T["LD%d" % o] for o in range(3)]
    CC = [slice(0, 32), slice(32, 64)]
    ALL = slice(0, 64)
    late = [[T.sem["a%d%d" % (o, c)] for c in range(2)] for o in range(2)]
    early = [T.sem.e10, T.sem.e11]
    full = topo.engines(core, peer[1])
    h0, h1 = full[:len(full) // 2], full[len(full) // 2:]

    def send(parts, *toks):
        need("g", *toks)
        tr = []
        for k, dst, src, rs, es in parts:
            rid, pid, _ = topo.addr(peer[k])
            tr.append(RemoteDMATransfer(dst_ids=[DstId(rid=rid, pnc=pid)], dma_engine_mask=bits(es), remote_sem=rs, src=src, dst=dst))
            sent[0] += len(es)
        g.remote_dma_fused(tr, local_sem=T.sem.sent)

    g.sync.dma_start(T.C8i[0:8, 0:64], T.px[:, :]).then_inc(T.sem.dC, 16)
    g.scalar.dma_start(T.C8i[0:8, 64:128], T.py[:, :]).then_inc(T.sem.dC, 16)
    g.sync.dma_start(T.Gt[:, :], T.green[:, :]).then_inc(T.sem.dG, 16)
    g.scalar.dma_start(T.QR[:, 0:64], T.q[:, :]).then_inc(T.sem.dQ, 16)
    g.scalar.dma_start(T.QR[:, 64:128], T.refl[:, :]).then_inc(T.sem.dQ, 16)

    onb = did("v", V.memset(T.ONB[:, :], 1.0))
    onf = did("v", V.memset(T.ONF[:, :], 1.0))
    rz = did("v", V.memset(T.RW[:, :, :, :], 0.0))
    mk = did("v", V.memset(T.MK[:, :], 1.0))
    need("v", mk)
    did("v", V.memset(T.MK[:, 0:192:3], 0.0))
    e8 = select(T.E8[0:8, :], T.ONB[0:8, 0:128], [[1, 128]], A.is_ge, 0, -16, onb)
    e8 = select(T.E8[0:8, :], T.E8[0:8, :], [[-1, 128]], A.is_ge, 15, 16, e8)
    z8 = select(T.Z8[0:8, :], T.ONB[0:8, :], [[1, 144]], A.is_equal, -15, -16)
    ib = select(T.IB[:, :], T.ONB[:, 0:128], [[-1, 128]], A.is_equal, 0, 1)
    for ah in range(2):
        iq = select(T.IQ[:, 64 * ah:64 * ah + 64], T.ONF[:, 0:64], [[-16, 2], [-1, 16], [-32, 2]], A.is_equal, -64 * ah, 1, onf)

    V.wait_ge(T.sem.dC, 32)
    c8 = vcopy(T.C8b[0:8, :], T.C8i[0:8, :])
    bc = mm(P[4][:, 0:128], T.E8[0:8, :], T.C8b[0:8, :], True, True, e8, c8)
    for a in range(16):
        bs = mm(P[5][:, 0:8], T.Z8[0:8, 15 - a:143 - a], T.C8b[0:8, a:128:16], a == 0, a == 15, z8)
    clt = vcopy(T.CLT[:, 0, :], P[4][:, 0:128], bc)
    sc = vcopy(T.SCf[:, 0:8], P[5][:, 0:8], bs)
    scy = did("v", V.tensor_scalar(T.SCf[:, 8:12], P[5][:, 4:8], 0.5, None, A.mult))
    send([(3, T.CLT[:, 1, :], T.CLT[:, 0, :], T.sem.crd1, full)], clt)
    send([(2, T.CLT[:, 2, :], T.CLT[:, 0, :], T.sem.crd2, h0), (1, T.CLT[:, 3, :], T.CLT[:, 0, :], T.sem.crd2, h1)])

    def offs_s(ks, *toks):
        need("s", *toks)
        for jj in range(4):
            t = did("s", S.activation(T.DX[:, ks, :, jj], T.CLT[:, ks, 0:64], ABS, bias=T.SCf[:, jj:jj + 1], scale=-1.0))
        return t

    def offs_v(ks, *toks):
        need("v", *toks)
        for jj in range(4):
            t = did("v", V.tensor_scalar(T.RA[:, ks, :, jj], T.CLT[:, ks, 64:128], T.SCf[:, 4 + jj:5 + jj], T.SCf[:, 8 + jj:9 + jj], A.max, A.subtract))
        return t

    def offs_t(k, ps, base, *toks):
        need("t", *toks)
        for jj in range(4):
            out = ps[:, base + jj:base + 256:4]
            mm(out, T.I64[:, :], T.DX[:, k, :, jj], True, False)
            mm(out, T.I2[:, :], T.RA[:, k, :, jj], False, False)
            t = mm(out, T.IN[:, :], T.CLT[:, k, 64:128], False, True)
        return t

    ox = offs_s(0, clt, sc)
    oy = offs_v(0, clt, sc, scy)
    need("v", ib)
    did("v", V.tensor_scalar(T.I64[:, :], T.IB[:, :], 64.0, None, A.mult))
    did("v", V.tensor_scalar(T.I2[:, :], T.IB[:, :], 2.0, None, A.mult))
    idn = did("v", V.tensor_scalar(T.IN[:, :], T.IB[:, :], -1.0, None, A.mult))
    ot = offs_t(0, P[6], 0, ox, oy, idn)
    off0 = vcopy(T.OFF[:, 0:256], P[6][:, 0:256], ot)

    def pieces(cols, hi, copiers):
        r1, w = T.R1[:, cols], T.WW[:, cols]
        need("v", hi)
        m = did("v", V.tensor_tensor(T.PC[:, 1, cols], w, T.PC[:, 0, cols], A.subtract))
        r = did("v", V.tensor_tensor(r1, w, T.PC[:, 0, cols], A.subtract))
        lo = vtt(T.PC[:, 2, cols], r1, T.PC[:, 1, cols], A.subtract, m, r)
        last = []
        for a in range(4):
            for jh in range(2):
                ah, a2 = divmod(a, 2)
                n0, p0 = 6 * a2 + 3 * ah, 64 * ah + 32 * jh
                src = T.PC[p0:p0 + 32, :, cols.start + a2:cols.stop:2]
                dst = T.RW[32 * a:32 * a + 32, n0:n0 + 3, jh, cols.start // 2:cols.stop // 2]
                last.append(copiers[a2](dst, src, lo))
        return last

    g.tensor.wait_ge(T.sem.dQ, 32)
    qt = mm(P[3][:, 0:128], T.QR[:, :], T.IQ[:, :], True, True, iq)
    for ah in range(2):
        qe = vcopy(T.WW[64 * ah:64 * ah + 64, :], P[3][0:64, ah * 64:ah * 64 + 64], qt)
    hi = vcopy(T.PC[:, 0, :], T.WW[:, :], qe)
    rw = pieces(ALL, hi, [gcopy([3, 32])] * 2) + [rz]
    for ah in range(2):
        vcopy(T.RT[64 * ah:64 * ah + 64, :], P[3][64:128, ah * 64:ah * 64 + 64])
    ip = select(T.IP[:, :], T.ONF[:, :], [[-64, 2], [-1, 64]], A.is_equal, 0, 1, *rw)

    def gather(q, k, u0, u1, *toks):
        a, b = k * 4096 + u0 * 512, k * 4096 + u1 * 512
        return (act if q == "s" else vcopy)(T.Mg[:, a:b], T.Gt[:, 0:4096].indirect(T.OFF[:, a // 16:b // 16]), *toks)

    def turn(k, u0, u1, *toks):
        a, b = k * 4096 + u0 * 512, k * 4096 + u1 * 512
        need("v", *toks)
        if k == 0:
            lo = 65 * 8 * u0
            z = did("v", V.memset(T.Mg[:, lo:min(lo + 65 * 8 * (u1 - u0), 4096):65], 0.0))
            need("v", z)
        return did("v", V.transpose(T.Tt[:, a:b], T.Mg[:, a:b]))

    def field(c, t0, nt, ps, p0, *toks, xs=range(16)):
        need("t", *toks)
        for x in xs:
            for jh in range(2):
                o = jh * 32 + 16 * c + x
                t = mm(ps[p0:p0 + nt, 12 * x:12 * x + 12], T.Tt[:, t0 * 64 + o:(t0 + nt) * 64:64], T.RW[:, :, jh, 16 * c + x], jh == 0, jh == 1)
        return t

    def block(k, b, toks):
        bank, p0 = ((4, 0), (0, 0), (0, 64), (2, 0))[k]
        return [field(c, 64 * k + 32 * b, 32, P[bank + c], p0 + 32 * b, *toks, *rw) for c in range(2)]

    nac = [0]

    def scan(np_, *banks):
        i = nac[0]
        nac[0] += 1
        for ps, a, b, tok in banks:
            need("v", tok)
            t = did("v", V.tensor_tensor_scan(T.SCN[0:np_, i, a:b], T.MK[0:np_, a:b], ps[0:np_, a:b], 0.0, A.mult, A.add))
        return i, t

    def part(i, h, ah):
        return T.SCN[64 * h:64 * h + 64, i, 3 * ah + 2:192:6]

    copier = {"v": vcopy, "s": act, "g": gcopy([32])}

    def evac(o, c, banks, slots):
        i, t = scan(64 * len(slots), *banks)
        res = {}
        for h, k, who in slots:
            res[k] = [copier[who[ah]]((LD if k == 0 else MS)[o][64 * ah:64 * ah + 64, k, CC[c]], part(i, h, ah), t) for ah in range(2)]
        return res

    def msg(o, cs, k, rs, es):
        return (k, LD[o][:, k, cs], MS[o][:, k, cs], rs, es)

    made, turned, tok, done, e12 = {}, {}, {("off", 0): off0}, {}, []
    crd = {1: T.sem.crd1, 2: T.sem.crd2}

    def share(q, plan):
        for what, k, u0, u1 in plan:
            if what == "gather":
                t = gather(q, k, u0, u1, tok["off", k])
                made.update({(k, u): t for u in range(u0, u1)})
            elif what == "turn":
                while any((k, u) not in made for u in range(u0, u1)):
                    next(scalar)
                t = turn(k, u0, u1, *[made[k, u] for u in range(u0, u1)])
                turned.update({(k, u): t for u in range(u0, u1)})
                for b in range(u0 // 4, (u1 + 3) // 4):
                    toks = [turned[k, u] for u in range(4 * b, 4 * b + 4) if (k, u) in turned]
                    if len(toks) == 4:
                        done[k] = block(k, b, toks)
            elif what == "places":
                qs[q].wait_ge(crd[k], len(full))
                tok[q, k] = (offs_s if q == "s" else offs_v)(slice(u0, u1))
            elif what == "offsets":
                while ("s", k) not in tok:
                    next(scalar)
                for i in range(u0, u1):
                    tok["t", k] = offs_t(i, P[5 + k], 256 * (i - u0), tok["s", k], tok["v", k], off0)
            elif what == "list":
                t = vcopy(T.OFF[:, 256 * u0:256 * u1], P[5 + k][:, 0:256 * (u1 - u0)], tok["t", k])
                tok.update({("off", i): t for i in range(u0, u1)})
            elif k == 3:
                c = u0
                e = evac(0, c, [(P[2 + c], 0, 192, done[3][c])], [(0, 3, COPIERS["3"])])
                send([msg(0, CC[c], 3, late[0][c], full)], *e[3])
            else:
                c = u0
                e = evac(0, c, [(P[c], 0, 192, max(done[1][c], done[2][c]))], [(0, 1, COPIERS["12"][0]), (1, 2, COPIERS["12"][1])])
                e12.extend(e[1] + e[2])
                if len(e12) == 8:
                    send([msg(0, ALL, 1, T.sem.e0, h0), msg(0, ALL, 2, T.sem.e0, h1)], *e12)
            yield what

    S.wait_ge(T.sem.dG, 16)
    V.wait_ge(T.sem.dG, 16)
    scalar = share("s", SPLAN)
    for _ in share("v", VPLAN):
        pass
    for _ in scalar:
        pass

    mine = {}

    def early_sum(o, c):
        if o == 0:
            i, t = scan(64, (P[4 + c], 0, 192, done[0][c]))
            if c == 0:
                V.wait_ge(T.sem.e0, len(full))
                need("v", vtt(T.EA[:, 0, :], LD[0][:, 1, :], LD[0][:, 2, :], A.add))
            need("v", t)
            for ah in range(2):
                r = slice(64 * ah, 64 * ah + 64)
                e = did("v", V.tensor_tensor(T.EB[r, 0, CC[c]], T.EA[r, 0, CC[c]], part(i, 0, ah), A.add))
            return e
        V.wait_ge(early[c], len(full))
        t = vtt(T.EA[:, 1, CC[c]], LD[1][:, 2, CC[c]], LD[1][:, 3, CC[c]], A.add)
        return vtt(T.EB[:, 1, CC[c]], T.EA[:, 1, CC[c]], LD[1][:, 0, CC[c]], A.add, t, *mine[c])

    banks = {1: [(6, 7, 0), (1, 2, 3)], 2: [(4, 5, 6), (7, 0, 1)]}
    e0 = [early_sum(0, c) for c in range(2)]
    for o in (1, 2):
        f = []
        for c in range(2):
            e = e0[c] if o == 1 else early_sum(1, c)
            V.wait_ge(late[o - 1][c], len(full))
            s = vtt(T.SS[:, o - 1, CC[c]], T.EB[:, o - 1, CC[c]], LD[o - 1][:, 3 if o == 1 else 1, CC[c]], A.add, e)
            need("v", s)
            did("v", V.tensor_tensor(T.PC[:, 0, CC[c]], T.SS[:, o - 1, CC[c]], T.RT[:, CC[c]], A.mult))
            hi = did("v", V.tensor_tensor(T.WW[:, CC[c]], T.SS[:, o - 1, CC[c]], T.RT[:, CC[c]], A.mult))
            r = pieces(CC[c], hi, [vcopy, act])
            bk = [P[b] for b in banks[o][c]]
            fb = field(c, 128, 128, bk[0], 0, *r)
            fa = [field(c, 0, 128, bk[1 + i], 0, xs=range(8 * i, 8 * i + 8)) for i in range(2)]
            f.append(([(bk[0], 0, 192, fb)], [(bk[1 + i], 96 * i, 96 * i + 96, fa[i]) for i in range(2)]))

        def first(c):
            return evac(o, c, f[c][0], [(0, 2, COPIERS["fb"][0]), (1, 3, COPIERS["fb"][1])])

        def second(c):
            return evac(o, c, f[c][1], [(1, 1, COPIERS["fa"][0]), (0, 0, COPIERS["fa"][1])])

        if o == 1:
            for c in range(2):
                e = first(c)
                send([msg(o, CC[c], 2, early[c], h0), msg(o, CC[c], 3, early[c], h1)], *e[2], *e[3])
                e = second(c)
                send([msg(o, CC[c], 1, late[o][c], full)], *e[1])
                mine[c] = e[0]
        else:
            ya = vtt(T.YA[:, :], T.SS[:, 0, :], T.SS[:, 1, :], A.add)
            e = [first(c) for c in range(2)]
            send([msg(o, ALL, 2, T.sem.e2, h0), msg(o, ALL, 3, T.sem.e2, h1)], *e[0][2], *e[0][3], *e[1][2], *e[1][3])
            e = [second(c) for c in range(2)]
            send([msg(o, ALL, 1, T.sem.a2, full)], *e[0][1], *e[1][1])
            own = vtt(LD[o][:, 0, :], LD[o][:, 0, :], T.YA[:, :], A.add, ya, *e[0][0], *e[1][0])

    V.wait_ge(T.sem.e2, len(full))
    t = vtt(T.EA[:, 2, :], LD[2][:, 2, :], LD[2][:, 3, :], A.add)
    e = vtt(T.EB[:, 2, :], T.EA[:, 2, :], LD[2][:, 0, :], A.add, t, own)
    V.wait_ge(T.sem.a2, len(full))
    for a2 in range(2):
        y = vtt(T.YT[:, 32 * a2:32 * a2 + 32], T.EB[:, 2, a2:64:2], LD[2][:, 1, a2:64:2], A.add, e)
    yt = mm(P[7][0:64, 256:384], T.YT[:, :], T.IP[:, :], True, True, y, ip)
    yb = vcopy(T.YB[0:64, :], P[7][0:64, 256:384], yt)
    need("y", yb)
    g.sync.dma_start(T.y[0:64, :], T.YB[0:64, 0:64]).then_inc(T.sem.dY, 16)
    need("s", yb)
    g.scalar.dma_start(T.y[64:128, :], T.YB[0:64, 64:128]).then_inc(T.sem.dY, 16)
    g.sync.wait_ge(T.sem.dY, 32)
    need("g", *[(q, cnt[q]) for q in cnt])
    g.wait_ge(T.sem.sent, sent[0])
